import numpy as np
import ml_dtypes


def mxq(x, axis, fmt="e4m3"):
    dtype, down = {"e4m3": (ml_dtypes.float8_e4m3fn, 7), "e5m2": (ml_dtypes.float8_e5m2, 14)}[fmt]
    v = np.moveaxis(np.asarray(x, np.float32).astype(ml_dtypes.bfloat16).astype(np.float64), axis, -1)
    blocks = v.reshape(v.shape[:-1] + (-1, 32))
    amax = np.abs(blocks).max(-1, keepdims=True)
    byte = np.maximum(np.where(amax > 0, np.frexp(amax)[1] - 1 + 127, 0) - down, 1)
    scale = np.exp2(byte - 127.0)
    codes = (blocks / scale).astype(np.float32).astype(dtype).astype(np.float64)
    return np.moveaxis((codes * scale).reshape(v.shape), -1, axis)


WIDE = False


def mx_kscale(k):
    if not WIDE:
        return np.ones(k)
    levels = np.array([10, -10, 5, -5, 0])
    if k % 512:
        return np.exp2(np.random.permutation(np.resize(levels, k // 32))).repeat(32)
    a = np.empty((k // 512, 16))
    for p in range(k // 512):
        a[p, :8] = np.random.permutation(np.resize(levels, 8))
        for g in range(8):
            far = levels[np.abs(levels - a[p, g]) >= 10]
            a[p, g + 8] = far[np.random.randint(len(far))]
    return np.exp2(a.ravel()).repeat(32)


def f64(x):
    return np.asarray(x).astype(np.float64)


def striped(idx):
    return np.tile(idx.reshape(-1, 16).T, (8, 1)).astype(np.uint16)


def unstriped(offs):
    return offs[:16].T.reshape(-1).astype(np.int64)


def pack_weight(w):
    k, n = w.shape
    w = f64(np.asarray(w, np.float32).astype(ml_dtypes.bfloat16)).reshape(k // 32, 32, n)
    amax = np.abs(w).max(1)
    byte = np.clip(np.where(amax > 0, np.frexp(amax)[1] - 1 + 127 - 7, 1), 1, 254)
    scaled = (w * np.exp2(127.0 - byte)[:, None, :]).reshape(k, n).astype(np.float32)
    words = np.ascontiguousarray(scaled.reshape(k // 512, 128, 4, n).transpose(0, 1, 3, 2)).astype(ml_dtypes.float8_e4m3fn).view(np.uint8)
    return words, np.ascontiguousarray(byte.astype(np.uint8).reshape(k // 512, 16, n))


def unpack_weight(words, scales):
    g, p, n, _ = words.shape
    vals = np.ascontiguousarray(words).view(ml_dtypes.float8_e4m3fn).astype(np.float64) * np.repeat(np.exp2(scales.astype(np.float64) - 127.0), 8, axis=1)[..., None]
    return vals.transpose(0, 1, 3, 2).reshape(g * 512, n)


def relu(v):
    return np.maximum(v, 0.0)


def sigmoid(v):
    return 1.0 / (1.0 + np.exp(-np.maximum(v, -700.0)))

def planes(y):
    n, m = y.shape
    v = y.astype(np.float32).astype(ml_dtypes.bfloat16).astype(np.float64).reshape(n // 32, 32, m)
    top = np.abs(v).max(1)
    byte = np.clip(np.where(top > 0, np.frexp(top)[1] - 1 + 127 - 7, 1), 1, 254)
    codes = (v * np.exp2(127.0 - byte)[:, None, :]).reshape(n, m).astype(np.float32).astype(ml_dtypes.float8_e4m3fn).view(np.uint8)
    words = codes.reshape(n // 512, 128, 4, m).transpose(0, 1, 3, 2)
    return np.ascontiguousarray(words), np.ascontiguousarray(byte.astype(np.uint8).reshape(n // 512, 16, m))


K, T, S, N = 512, 1024, 512, 512


def setup_inputs():
    n = np.random.standard_normal
    s = mx_kscale(K)[:, None]
    packed_xT = pack_weight(n((K, T)) * s)
    return {
        "x_words": packed_xT[0],
        "x_scales": packed_xT[1],
        "res": n((N, T)).astype(np.float32),
        "w1": (n((K, N)) / np.sqrt(K) / s).astype(np.float32),
        "w2": (n((K, N)) / np.sqrt(K) / s).astype(np.float32),
        "offs": striped(np.random.permutation(T)[:S]),
    }


def reference(x_words, x_scales, res, w1, w2, offs):
    r = f64(res)[:, unstriped(offs)]
    xq = unpack_weight(x_words, x_scales)[:, unstriped(offs)]
    g = sigmoid(mxq(f64(w2), 0, "e4m3").T @ xq)
    y = relu(mxq(f64(w1), 0, "e4m3").T @ xq)
    out_0 = r + g * (y - r)
    return (out_0,) + planes(out_0)

@@ -1,0 +1,177 @@
+from contextlib import ExitStack
+
+import concourse.mybir as mybir
+
+K, T, S, N = 512, 1024, 512, 512
+FLOPS = 2 * 2 * K * N * S
+
+F32 = mybir.dt.float32
+BF16 = mybir.dt.bfloat16
+I32 = mybir.dt.int32
+U32 = mybir.dt.uint32
+U16 = mybir.dt.uint16
+U8 = mybir.dt.uint8
+FP8X4 = mybir.dt.float8_e4m3fn_x4
+ALU = mybir.AluOpType
+ACT = mybir.ActivationFunctionType
+
+P = 128
+PACK = 4
+HALF = N // 2
+CHUNK = 128
+CHUNKS = S // CHUNK
+
+
+def tile_picked_highway_relu_po_kernel(tc, x_words, x_scales, res, w1, w2, offs, out_0, out_1, out_2):
+    nc = tc.nc
+    with ExitStack() as ctx:
+        pool = ctx.enter_context(tc.tile_pool(name="held", bufs=1))
+        psum = ctx.enter_context(tc.psum_pool(name="psum", bufs=1))
+
+        offsets = pool.tile([P, S // 16], U16, name="offsets")
+        nc.sync.dma_start(offsets[:], offs)
+
+        scale_window = pool.tile([P, T], U8, name="scale_window")
+        warm_in = pool.tile([P, 1], F32, name="warm_in")
+        warm_out = pool.tile([P, 1], F32, name="warm_out")
+        nc.vector.memset(warm_in[:], 0.0)
+        nc.scalar.activation(warm_out[:], warm_in[:], ACT.Sigmoid)
+
+        def load_weight_half(w, name, h, room=None):
+            if room is None:
+                own = pool.tile([P, PACK * HALF], F32, name=name + "_raw%d" % h)
+                room = own[:]
+            raw = room.rearrange("p (j c) -> p j c", j=PACK)
+            nc.sync.dma_start(raw, w.rearrange("(p j) c -> p j c", j=PACK)[:, :, h * HALF : (h + 1) * HALF])
+            return raw
+
+        def load_res(t):
+            window = pool.tile([P, T], F32, name="res_window%d" % t)
+            nc.sync.dma_start(window[:], res.rearrange("(p t) c -> p t c", t=PACK)[:, t, :])
+            return window
+
+        word_window = pool.tile([P, T], U32, name="word_window")
+        nc.sync.dma_start(word_window[:].bitcast(I32), x_words[0].rearrange("p c r -> p (c r)").bitcast(I32))
+        for q in range(4):
+            rows = x_scales[0, 4 * q : 4 * q + 4, :].bitcast(I32)
+            nc.sync.dma_start(scale_window[32 * q : 32 * q + 32, :].bitcast(I32), rows.unsqueeze(0).broadcast_to([8, 4, T // 4]))
+        w2_raw = [load_weight_half(w2, "w2", h) for h in range(2)]
+        res_window = [load_res(t) for t in range(2)]
+        gate_rows = pool.tile([P, PACK * S], F32, name="gate_rows")
+        gate = gate_rows[:].rearrange("p (t s) -> p t s", t=PACK)
+        w1_raw = [load_weight_half(w1, "w1", 0), load_weight_half(w1, "w1", 1, gate_rows[:, 2 * S :])]
+        res_window.extend([load_res(t) for t in range(2, PACK)])
+
+        def deal(copy, grouped, raw, h):
+            dealt = grouped[:].rearrange("p (t m j) -> p m j t", t=PACK, j=PACK)
+            copy(dealt[:, h * HALF // PACK : (h + 1) * HALF // PACK], raw.rearrange("p j (m t) -> p m j t", t=PACK))
+
+        def quantise_weight(grouped, name):
+            codes = pool.tile([P, N], U32, name=name + "_codes", align_bytes=64)
+            scales = pool.tile([P, N], U8, name=name + "_scales", align_bytes=64)
+            nc.vector.quantize_mx(codes[:].bitcast(FP8X4), scales[:], grouped[:])
+            return codes, scales
+
+        x_code = pool.tile([P, S], U32, name="x_code", align_bytes=64)
+        nc.vector.tensor_copy(x_code[:], word_window[:].indirect(offsets[:]))
+        x_scale = pool.tile([P, S], U8, name="x_scale", align_bytes=64)
+        nc.vector.tensor_copy(x_scale[:], scale_window[:].indirect(offsets[:]))
+
+        w2_grouped = pool.tile([P, N * PACK], BF16, name="w2_grouped", align_bytes=64)
+        deal(nc.scalar.copy, w2_grouped, w2_raw[0], 0)
+        deal(nc.vector.tensor_copy, w2_grouped, w2_raw[1], 1)
+        w2_codes, w2_scales = quantise_weight(w2_grouped, "w2")
+
+        def make_gate(t):
+            cols = slice(t * P, (t + 1) * P)
+            bank = psum.tile([P, S], F32, name="gate_bank%d" % t)
+            nc.tensor.matmul_mx(
+                bank[:],
+                lhsT=w2_codes[:, cols].bitcast(FP8X4),
+                lhsT_scale=w2_scales[:, cols],
+                rhs=x_code[:].bitcast(FP8X4),
+                rhs_scale=x_scale[:],
+                start=True,
+                stop=True,
+            )
+            nc.scalar.activation(gate[:, t, :], bank[:], ACT.Sigmoid)
+
+        make_gate(0)
+        make_gate(1)
+        passed = pool.tile([P, PACK, S], F32, name="passed")
+        carried = pool.tile([P, PACK, S], F32, name="carried")
+
+        def gather_res(t):
+            nc.vector.tensor_copy(passed[:, t, :], res_window[t][:].indirect(offsets[:]))
+
+        def carry(t):
+            nc.vector.scalar_tensor_tensor(carried[:, t, :], gate[:, t, :], 1.0, passed[:, t, :], ALU.subtract, ALU.mult)
+
+        gather_res(0)
+        gather_res(1)
+        carry(0)
+        carry(1)
+
+        w1_grouped = pool.tile([P, N * PACK], BF16, name="w1_grouped", align_bytes=64)
+        deal(nc.scalar.copy, w1_grouped, w1_raw[0], 0)
+        deal(nc.scalar.copy, w1_grouped, w1_raw[1], 1)
+        make_gate(2)
+        make_gate(3)
+        gather_res(2)
+        w1_codes, w1_scales = quantise_weight(w1_grouped, "w1")
+        carry(2)
+        gather_res(3)
+
+        out_codes = pool.tile([P, S], U32, name="out_codes", align_bytes=64)
+        out_scales = pool.tile([P, S], U8, name="out_scales", align_bytes=64)
+        out_rows = out_0.rearrange("(p t) s -> p t s", t=PACK)
+        out_words = out_1[0].rearrange("p s r -> p (s r)").bitcast(I32)
+
+        def gated_product(c):
+            tokens = slice(c * CHUNK, (c + 1) * CHUNK)
+            bank = psum.tile([P, PACK, CHUNK], F32, name="layer_bank%d" % c)
+            for t in range(PACK):
+                cols = slice(t * P, (t + 1) * P)
+                nc.tensor.matmul_mx(
+                    bank[:, t, :],
+                    lhsT=w1_codes[:, cols].bitcast(FP8X4),
+                    lhsT_scale=w1_scales[:, cols],
+                    rhs=x_code[:, tokens].bitcast(FP8X4),
+                    rhs_scale=x_scale[:, tokens],
+                    start=True,
+                    stop=True,
+                )
+            gated = pool.tile([P, PACK, CHUNK], F32, name="gated%d" % c)
+            nc.vector.scalar_tensor_tensor(gated[:], bank[:], 0.0, gate[:, :, tokens], ALU.max, ALU.mult)
+            return gated
+
+        def combine(c, gated):
+            tokens = slice(c * CHUNK, (c + 1) * CHUNK)
+            result = pool.tile([P, PACK, CHUNK], F32, name="result%d" % c)
+            nc.vector.tensor_tensor(result[:], gated[:], carried[:, :, tokens], ALU.subtract)
+            nc.sync.dma_start(out_rows[:, :, tokens], result[:])
+            grouped = pool.tile([P, CHUNK, PACK], BF16, name="out_grouped%d" % c, align_bytes=64)
+            nc.scalar.copy(
+                grouped[:].rearrange("p (c i) t -> p c t i", i=4),
+                result[:].rearrange("p t (c i) -> p c t i", i=4),
+            )
+            return grouped
+
+        def quantise_out(c, grouped):
+            tokens = slice(c * CHUNK, (c + 1) * CHUNK)
+            nc.vector.quantize_mx(out_codes[:, tokens].bitcast(FP8X4), out_scales[:, tokens], grouped[:].rearrange("p s t -> p (s t)"))
+            nc.sync.dma_start(out_words[:, tokens], out_codes[:, tokens].bitcast(I32))
+
+        gated = [gated_product(0)]
+        carry(3)
+        grouped = []
+        for c in range(CHUNKS):
+            if c + 1 < CHUNKS:
+                gated.append(gated_product(c + 1))
+            grouped.append(combine(c, gated[c]))
+            if c > 0:
+                quantise_out(c - 1, grouped[c - 1])
+        quantise_out(CHUNKS - 1, grouped[CHUNKS - 1])
+        for q in range(4):
+            queue = nc.scalar if q % 2 else nc.sync
+            queue.dma_start(out_2[0, 4 * q : 4 * q + 4, :].bitcast(I32), out_scales[32 * q : 32 * q + 4, :].bitcast(I32))

@@ -20,6 +20,7 @@ PACK = 4
 HALF = N // 2
 CHUNK = 128
 CHUNKS = S // CHUNK
+ROOM = PACK * HALF
 
 
 def tile_picked_highway_relu_po_kernel(tc, x_words, x_scales, res, w1, w2, offs, out_0, out_1, out_2):
@@ -29,7 +30,6 @@ def tile_picked_highway_relu_po_kernel(tc, x_words, x_scales, res, w1, w2, offs,
         psum = ctx.enter_context(tc.psum_pool(name="psum", bufs=1))
 
         offsets = pool.tile([P, S // 16], U16, name="offsets")
-        nc.sync.dma_start(offsets[:], offs)
 
         scale_window = pool.tile([P, T], U8, name="scale_window")
         warm_in = pool.tile([P, 1], F32, name="warm_in")
@@ -37,10 +37,7 @@ def tile_picked_highway_relu_po_kernel(tc, x_words, x_scales, res, w1, w2, offs,
         nc.vector.memset(warm_in[:], 0.0)
         nc.scalar.activation(warm_out[:], warm_in[:], ACT.Sigmoid)
 
-        def load_weight_half(w, name, h, room=None):
-            if room is None:
-                own = pool.tile([P, PACK * HALF], F32, name=name + "_raw%d" % h)
-                room = own[:]
+        def load_weight_half(w, room, h):
             raw = room.rearrange("p (j c) -> p j c", j=PACK)
             nc.sync.dma_start(raw, w.rearrange("(p j) c -> p j c", j=PACK)[:, :, h * HALF : (h + 1) * HALF])
             return raw
@@ -52,19 +49,24 @@ def tile_picked_highway_relu_po_kernel(tc, x_words, x_scales, res, w1, w2, offs,
 
         word_window = pool.tile([P, T], U32, name="word_window")
         nc.sync.dma_start(word_window[:].bitcast(I32), x_words[0].rearrange("p c r -> p (c r)").bitcast(I32))
+        nc.sync.dma_start(offsets[:], offs)
         for q in range(4):
             rows = x_scales[0, 4 * q : 4 * q + 4, :].bitcast(I32)
             nc.sync.dma_start(scale_window[32 * q : 32 * q + 32, :].bitcast(I32), rows.unsqueeze(0).broadcast_to([8, 4, T // 4]))
-        w2_raw = [load_weight_half(w2, "w2", h) for h in range(2)]
+        w2_rooms = [pool.tile([P, ROOM], F32, name="w2_room%d" % h) for h in range(2)]
+        w2_raw = [load_weight_half(w2, w2_rooms[h][:], h) for h in range(2)]
+        rooms = pool.tile([P, PACK * ROOM], F32, name="rooms")
+        gate = rooms[:].rearrange("p (t s) -> p t s", t=PACK)[:, :, :S]
         res_window = [load_res(t) for t in range(2)]
-        gate_rows = pool.tile([P, PACK * S], F32, name="gate_rows")
-        gate = gate_rows[:].rearrange("p (t s) -> p t s", t=PACK)
-        w1_raw = [load_weight_half(w1, "w1", 0), load_weight_half(w1, "w1", 1, gate_rows[:, 2 * S :])]
-        res_window.extend([load_res(t) for t in range(2, PACK)])
+        w1_raw = [load_weight_half(w1, rooms[:, 2 * ROOM : 3 * ROOM], 0)]
+        res_window.append(load_res(2))
+        w1_raw.append(load_weight_half(w1, rooms[:, 3 * ROOM :], 1))
+        res_window.append(load_res(3))
 
-        def deal(copy, grouped, raw, h):
+        def deal(copy, grouped, raw, h, lo=0, hi=HALF // PACK):
             dealt = grouped[:].rearrange("p (t m j) -> p m j t", t=PACK, j=PACK)
-            copy(dealt[:, h * HALF // PACK : (h + 1) * HALF // PACK], raw.rearrange("p j (m t) -> p m j t", t=PACK))
+            first = h * HALF // PACK
+            copy(dealt[:, first + lo : first + hi], raw.rearrange("p j (m t) -> p m j t", t=PACK)[:, lo:hi])
 
         def quantise_weight(grouped, name):
             codes = pool.tile([P, N], U32, name=name + "_codes", align_bytes=64)
@@ -98,29 +100,34 @@ def tile_picked_highway_relu_po_kernel(tc, x_words, x_scales, res, w1, w2, offs,
 
         make_gate(0)
         make_gate(1)
-        passed = pool.tile([P, PACK, S], F32, name="passed")
+        passed = []
         carried = pool.tile([P, PACK, S], F32, name="carried")
 
-        def gather_res(t):
-            nc.vector.tensor_copy(passed[:, t, :], res_window[t][:].indirect(offsets[:]))
+        def gather_res(t, tag):
+            picked = pool.tile([P, S], F32, name="passed%d" % t, tag=tag, align_bytes=64)
+            nc.vector.tensor_copy(picked[:], res_window[t][:].indirect(offsets[:]))
+            passed.append(picked)
 
         def carry(t):
-            nc.vector.scalar_tensor_tensor(carried[:, t, :], gate[:, t, :], 1.0, passed[:, t, :], ALU.subtract, ALU.mult)
+            nc.vector.scalar_tensor_tensor(carried[:, t, :], gate[:, t, :], 1.0, passed[t][:], ALU.subtract, ALU.mult)
 
-        gather_res(0)
-        gather_res(1)
+        gather_res(0, "passed0")
+        gather_res(1, "passed1")
         carry(0)
         carry(1)
 
-        w1_grouped = pool.tile([P, N * PACK], BF16, name="w1_grouped", align_bytes=64)
+        w1_grouped = pool.tile([P, N * PACK], BF16, name="w1_grouped", tag="w1_grouped", align_bytes=64)
         deal(nc.scalar.copy, w1_grouped, w1_raw[0], 0)
-        deal(nc.scalar.copy, w1_grouped, w1_raw[1], 1)
         make_gate(2)
-        make_gate(3)
-        gather_res(2)
-        w1_codes, w1_scales = quantise_weight(w1_grouped, "w1")
+        gather_res(2, "passed2")
         carry(2)
-        gather_res(3)
+        deal(nc.scalar.copy, w1_grouped, w1_raw[1], 1)
+        make_gate(3)
+        w1_codes, w1_scales = quantise_weight(w1_grouped, "w1")
+        shut = pool.tile([P, S], F32, name="shut")
+        nc.scalar.activation(shut[:], gate[:, 3, :], ACT.Identity, bias=-1.0)
+        gather_res(3, "w1_grouped")
+        nc.gpsimd.tensor_tensor(carried[:, 3, :], shut[:], passed[3][:], ALU.mult)
 
         out_codes = pool.tile([P, S], U32, name="out_codes", align_bytes=64)
         out_scales = pool.tile([P, S], U8, name="out_scales", align_bytes=64)
@@ -145,33 +152,29 @@ def tile_picked_highway_relu_po_kernel(tc, x_words, x_scales, res, w1, w2, offs,
             nc.vector.scalar_tensor_tensor(gated[:], bank[:], 0.0, gate[:, :, tokens], ALU.max, ALU.mult)
             return gated
 
-        def combine(c, gated):
+        def combine(c, gated, grouped):
             tokens = slice(c * CHUNK, (c + 1) * CHUNK)
             result = pool.tile([P, PACK, CHUNK], F32, name="result%d" % c)
-            nc.vector.tensor_tensor(result[:], gated[:], carried[:, :, tokens], ALU.subtract)
+            engine = nc.gpsimd if c == 0 else nc.vector
+            engine.tensor_tensor(result[:], gated[:], carried[:, :, tokens], ALU.subtract)
             nc.sync.dma_start(out_rows[:, :, tokens], result[:])
-            grouped = pool.tile([P, CHUNK, PACK], BF16, name="out_grouped%d" % c, align_bytes=64)
             nc.scalar.copy(
-                grouped[:].rearrange("p (c i) t -> p c t i", i=4),
+                grouped.rearrange("p (c i t) -> p c t i", i=4, t=PACK),
                 result[:].rearrange("p t (c i) -> p c t i", i=4),
             )
-            return grouped
 
-        def quantise_out(c, grouped):
-            tokens = slice(c * CHUNK, (c + 1) * CHUNK)
-            nc.vector.quantize_mx(out_codes[:, tokens].bitcast(FP8X4), out_scales[:, tokens], grouped[:].rearrange("p s t -> p (s t)"))
+        def quantise_out(tokens, grouped):
+            nc.vector.quantize_mx(out_codes[:, tokens].bitcast(FP8X4), out_scales[:, tokens], grouped[:])
             nc.sync.dma_start(out_words[:, tokens], out_codes[:, tokens].bitcast(I32))
 
-        gated = [gated_product(0)]
-        carry(3)
-        grouped = []
+        runs = [(0, 2), (2, 3), (3, 4)]
+        grouped = [pool.tile([P, (b - a) * CHUNK * PACK], BF16, name="out_grouped%d" % a, align_bytes=64) for a, b in runs]
+        room = [tile[:, i * CHUNK * PACK : (i + 1) * CHUNK * PACK] for tile, (a, b) in zip(grouped, runs) for i in range(b - a)]
+        gated = [gated_product(c) for c in range(CHUNKS)]
         for c in range(CHUNKS):
-            if c + 1 < CHUNKS:
-                gated.append(gated_product(c + 1))
-            grouped.append(combine(c, gated[c]))
-            if c > 0:
-                quantise_out(c - 1, grouped[c - 1])
-        quantise_out(CHUNKS - 1, grouped[CHUNKS - 1])
+            combine(c, gated[c], room[c])
+        for tile, (a, b) in zip(grouped, runs):
+            quantise_out(slice(a * CHUNK, b * CHUNK), tile)
         for q in range(4):
             queue = nc.scalar if q % 2 else nc.sync
             queue.dma_start(out_2[0, 4 * q : 4 * q + 4, :].bitcast(I32), out_scales[32 * q : 32 * q + 4, :].bitcast(I32))

@@ -18,8 +18,8 @@ ACT = mybir.ActivationFunctionType
 P = 128
 PACK = 4
 HALF = N // 2
-CHUNK = 128
-CHUNKS = S // CHUNK
+SPAN = S // 2
+SCALAR_SHARE = 128
 ROOM = PACK * HALF
 
 
@@ -32,6 +32,7 @@ def tile_picked_highway_relu_po_kernel(tc, x_words, x_scales, res, w1, w2, offs,
         offsets = pool.tile([P, S // 16], U16, name="offsets")
 
         scale_window = pool.tile([P, T], U8, name="scale_window")
+        nc.vector.memset(scale_window[:].bitcast(I32), 0)
         warm_in = pool.tile([P, 1], F32, name="warm_in")
         warm_out = pool.tile([P, 1], F32, name="warm_out")
         nc.vector.memset(warm_in[:], 0.0)
@@ -52,7 +53,7 @@ def tile_picked_highway_relu_po_kernel(tc, x_words, x_scales, res, w1, w2, offs,
         nc.sync.dma_start(offsets[:], offs)
         for q in range(4):
             rows = x_scales[0, 4 * q : 4 * q + 4, :].bitcast(I32)
-            nc.sync.dma_start(scale_window[32 * q : 32 * q + 32, :].bitcast(I32), rows.unsqueeze(0).broadcast_to([8, 4, T // 4]))
+            nc.sync.dma_start(scale_window[32 * q : 32 * q + 4, :].bitcast(I32), rows)
         w2_rooms = [pool.tile([P, ROOM], F32, name="w2_room%d" % h) for h in range(2)]
         w2_raw = [load_weight_half(w2, w2_rooms[h][:], h) for h in range(2)]
         rooms = pool.tile([P, PACK * ROOM], F32, name="rooms")
@@ -134,47 +135,54 @@ def tile_picked_highway_relu_po_kernel(tc, x_words, x_scales, res, w1, w2, offs,
         out_rows = out_0.rearrange("(p t) s -> p t s", t=PACK)
         out_words = out_1[0].rearrange("p s r -> p (s r)").bitcast(I32)
 
-        def gated_product(c):
-            tokens = slice(c * CHUNK, (c + 1) * CHUNK)
-            bank = psum.tile([P, PACK, CHUNK], F32, name="layer_bank%d" % c)
-            for t in range(PACK):
-                cols = slice(t * P, (t + 1) * P)
-                nc.tensor.matmul_mx(
-                    bank[:, t, :],
-                    lhsT=w1_codes[:, cols].bitcast(FP8X4),
-                    lhsT_scale=w1_scales[:, cols],
-                    rhs=x_code[:, tokens].bitcast(FP8X4),
-                    rhs_scale=x_scale[:, tokens],
-                    start=True,
-                    stop=True,
-                )
-            gated = pool.tile([P, PACK, CHUNK], F32, name="gated%d" % c)
-            nc.vector.scalar_tensor_tensor(gated[:], bank[:], 0.0, gate[:, :, tokens], ALU.max, ALU.mult)
-            return gated
+        gated = pool.tile([P, PACK, S], F32, name="gated")
+        for t in range(PACK):
+            cols = slice(t * P, (t + 1) * P)
+            bank = psum.tile([P, S], F32, name="layer_bank%d" % t)
+            nc.tensor.matmul_mx(
+                bank[:],
+                lhsT=w1_codes[:, cols].bitcast(FP8X4),
+                lhsT_scale=w1_scales[:, cols],
+                rhs=x_code[:].bitcast(FP8X4),
+                rhs_scale=x_scale[:],
+                start=True,
+                stop=True,
+            )
+            nc.vector.scalar_tensor_tensor(gated[:, t, :], bank[:], 0.0, gate[:, t, :], ALU.max, ALU.mult)
 
-        def combine(c, gated, grouped):
-            tokens = slice(c * CHUNK, (c + 1) * CHUNK)
-            result = pool.tile([P, PACK, CHUNK], F32, name="result%d" % c)
-            engine = nc.gpsimd if c == 0 else nc.vector
-            engine.tensor_tensor(result[:], gated[:], carried[:, :, tokens], ALU.subtract)
-            nc.sync.dma_start(out_rows[:, :, tokens], result[:])
-            nc.scalar.copy(
-                grouped.rearrange("p (c i t) -> p c t i", i=4, t=PACK),
-                result[:].rearrange("p t (c i) -> p c t i", i=4),
+        result = [pool.tile([P, PACK, SPAN], F32, name="result%d" % h) for h in range(2)]
+        grouped = [pool.tile([P, SPAN, PACK], BF16, name="out_grouped%d" % h, align_bytes=64) for h in range(2)]
+
+        def combine(engine, planes, h, pieces):
+            width = SPAN // pieces
+            for first in range(0, SPAN, width):
+                tokens = slice(h * SPAN + first, h * SPAN + first + width)
+                engine.tensor_tensor(
+                    result[h][:, planes, first : first + width], gated[:, planes, tokens], carried[:, planes, tokens], ALU.subtract
+                )
+            nc.sync.dma_start(out_rows[:, planes, h * SPAN : (h + 1) * SPAN], result[h][:, planes, :])
+
+        def interleave(copy, h, part):
+            copy(
+                grouped[h][:, part, :].rearrange("p (c i) t -> p c t i", i=4),
+                result[h][:, :, part].rearrange("p t (c i) -> p c t i", i=4),
             )
 
-        def quantise_out(tokens, grouped):
-            nc.vector.quantize_mx(out_codes[:, tokens].bitcast(FP8X4), out_scales[:, tokens], grouped[:])
+        def quantise_out(h):
+            tokens = slice(h * SPAN, (h + 1) * SPAN)
+            nc.vector.quantize_mx(out_codes[:, tokens].bitcast(FP8X4), out_scales[:, tokens], grouped[h][:].rearrange("p s t -> p (s t)"))
             nc.sync.dma_start(out_words[:, tokens], out_codes[:, tokens].bitcast(I32))
 
-        runs = [(0, 2), (2, 3), (3, 4)]
-        grouped = [pool.tile([P, (b - a) * CHUNK * PACK], BF16, name="out_grouped%d" % a, align_bytes=64) for a, b in runs]
-        room = [tile[:, i * CHUNK * PACK : (i + 1) * CHUNK * PACK] for tile, (a, b) in zip(grouped, runs) for i in range(b - a)]
-        gated = [gated_product(c) for c in range(CHUNKS)]
-        for c in range(CHUNKS):
-            combine(c, gated[c], room[c])
-        for tile, (a, b) in zip(grouped, runs):
-            quantise_out(slice(a * CHUNK, b * CHUNK), tile)
+        for h in range(2):
+            combine(nc.gpsimd, slice(0, 1), h, 1)
+        combine(nc.vector, slice(1, PACK), 0, 2)
+        combine(nc.vector, slice(1, PACK), 1, 1)
+        interleave(nc.scalar.copy, 0, slice(0, SPAN // 2))
+        interleave(nc.scalar.copy, 0, slice(SPAN // 2, SPAN))
+        interleave(nc.scalar.copy, 1, slice(0, SCALAR_SHARE))
+        quantise_out(0)
+        interleave(nc.vector.tensor_copy, 1, slice(SCALAR_SHARE, SPAN))
+        quantise_out(1)
         for q in range(4):
             queue = nc.scalar if q % 2 else nc.sync
             queue.dma_start(out_2[0, 4 * q : 4 * q + 4, :].bitcast(I32), out_scales[32 * q : 32 * q + 4, :].bitcast(I32))

@@ -19,7 +19,8 @@ P = 128
 PACK = 4
 HALF = N // 2
 SPAN = S // 2
-SCALAR_SHARE = 128
+SCALAR_SHARE = 160
+SPLIT = 40
 ROOM = PACK * HALF
 
 
@@ -56,12 +57,11 @@ def tile_picked_highway_relu_po_kernel(tc, x_words, x_scales, res, w1, w2, offs,
             nc.sync.dma_start(scale_window[32 * q : 32 * q + 4, :].bitcast(I32), rows)
         w2_rooms = [pool.tile([P, ROOM], F32, name="w2_room%d" % h) for h in range(2)]
         w2_raw = [load_weight_half(w2, w2_rooms[h][:], h) for h in range(2)]
-        rooms = pool.tile([P, PACK * ROOM], F32, name="rooms")
-        gate = rooms[:].rearrange("p (t s) -> p t s", t=PACK)[:, :, :S]
+        w1_rooms = [pool.tile([P, ROOM], F32, name="w1_room%d" % h, tag="w1_room%d" % h) for h in range(2)]
         res_window = [load_res(t) for t in range(2)]
-        w1_raw = [load_weight_half(w1, rooms[:, 2 * ROOM : 3 * ROOM], 0)]
+        w1_raw = [load_weight_half(w1, w1_rooms[0][:], 0)]
         res_window.append(load_res(2))
-        w1_raw.append(load_weight_half(w1, rooms[:, 3 * ROOM :], 1))
+        w1_raw.append(load_weight_half(w1, w1_rooms[1][:], 1))
         res_window.append(load_res(3))
 
         def deal(copy, grouped, raw, h, lo=0, hi=HALF // PACK):
@@ -69,10 +69,13 @@ def tile_picked_highway_relu_po_kernel(tc, x_words, x_scales, res, w1, w2, offs,
             first = h * HALF // PACK
             copy(dealt[:, first + lo : first + hi], raw.rearrange("p j (m t) -> p m j t", t=PACK)[:, lo:hi])
 
-        def quantise_weight(grouped, name):
+        def quantise_weight(grouped, name, pieces):
             codes = pool.tile([P, N], U32, name=name + "_codes", align_bytes=64)
             scales = pool.tile([P, N], U8, name=name + "_scales", align_bytes=64)
-            nc.vector.quantize_mx(codes[:].bitcast(FP8X4), scales[:], grouped[:])
+            width = N // pieces
+            for first in range(0, N, width):
+                cols = slice(first, first + width)
+                nc.vector.quantize_mx(codes[:, cols].bitcast(FP8X4), scales[:, cols], grouped[:, first * PACK : (first + width) * PACK])
             return codes, scales
 
         x_code = pool.tile([P, S], U32, name="x_code", align_bytes=64)
@@ -83,9 +86,11 @@ def tile_picked_highway_relu_po_kernel(tc, x_words, x_scales, res, w1, w2, offs,
         w2_grouped = pool.tile([P, N * PACK], BF16, name="w2_grouped", align_bytes=64)
         deal(nc.scalar.copy, w2_grouped, w2_raw[0], 0)
         deal(nc.vector.tensor_copy, w2_grouped, w2_raw[1], 1)
-        w2_codes, w2_scales = quantise_weight(w2_grouped, "w2")
+        w2_codes, w2_scales = quantise_weight(w2_grouped, "w2", 2)
 
-        def make_gate(t):
+        gate_banks = []
+        shut = []
+        for t in range(PACK):
             cols = slice(t * P, (t + 1) * P)
             bank = psum.tile([P, S], F32, name="gate_bank%d" % t)
             nc.tensor.matmul_mx(
@@ -97,38 +102,36 @@ def tile_picked_highway_relu_po_kernel(tc, x_words, x_scales, res, w1, w2, offs,
                 start=True,
                 stop=True,
             )
-            nc.scalar.activation(gate[:, t, :], bank[:], ACT.Sigmoid)
+            gate_banks.append(bank)
 
-        make_gate(0)
-        make_gate(1)
-        passed = []
+        for t in range(PACK - 1):
+            closed = pool.tile([P, S], F32, name="shut%d" % t)
+            nc.scalar.activation(closed[:], gate_banks[t][:], ACT.Sigmoid, scale=-1.0)
+            shut.append(closed)
+
         carried = pool.tile([P, PACK, S], F32, name="carried")
 
         def gather_res(t, tag):
             picked = pool.tile([P, S], F32, name="passed%d" % t, tag=tag, align_bytes=64)
             nc.vector.tensor_copy(picked[:], res_window[t][:].indirect(offsets[:]))
-            passed.append(picked)
+            return picked
 
-        def carry(t):
-            nc.vector.scalar_tensor_tensor(carried[:, t, :], gate[:, t, :], 1.0, passed[t][:], ALU.subtract, ALU.mult)
-
-        gather_res(0, "passed0")
-        gather_res(1, "passed1")
-        carry(0)
-        carry(1)
+        first_passed = gather_res(0, "passed0")
+        nc.vector.tensor_tensor(carried[:, 0, :], first_passed[:], shut[0][:], ALU.mult)
+        for t in (1, 2):
+            nc.vector.tensor_tensor(carried[:, t, :], res_window[t][:].indirect(offsets[:]), shut[t][:], ALU.mult)
 
         w1_grouped = pool.tile([P, N * PACK], BF16, name="w1_grouped", tag="w1_grouped", align_bytes=64)
         deal(nc.scalar.copy, w1_grouped, w1_raw[0], 0)
-        make_gate(2)
-        gather_res(2, "passed2")
-        carry(2)
-        deal(nc.scalar.copy, w1_grouped, w1_raw[1], 1)
-        make_gate(3)
-        w1_codes, w1_scales = quantise_weight(w1_grouped, "w1")
-        shut = pool.tile([P, S], F32, name="shut")
-        nc.scalar.activation(shut[:], gate[:, 3, :], ACT.Identity, bias=-1.0)
-        gather_res(3, "w1_grouped")
-        nc.gpsimd.tensor_tensor(carried[:, 3, :], shut[:], passed[3][:], ALU.mult)
+        deal(nc.scalar.copy, w1_grouped, w1_raw[1], 1, 0, SPLIT)
+        deal(nc.vector.tensor_copy, w1_grouped, w1_raw[1], 1, SPLIT, HALF // PACK)
+        w1_codes, w1_scales = quantise_weight(w1_grouped, "w1", 1)
+        gate = pool.tile([P, PACK + 1, S], F32, name="gate", tag="w1_room1")
+        nc.scalar.activation(gate[:, PACK, :], gate_banks[PACK - 1][:], ACT.Sigmoid, scale=-1.0)
+        for t in range(PACK):
+            nc.scalar.activation(gate[:, t, :], gate_banks[t][:], ACT.Sigmoid)
+        last_passed = gather_res(3, "w1_grouped")
+        nc.gpsimd.tensor_tensor(carried[:, 3, :], last_passed[:], gate[:, PACK, :], ALU.mult)
 
         out_codes = pool.tile([P, S], U32, name="out_codes", align_bytes=64)
         out_scales = pool.tile([P, S], U8, name="out_scales", align_bytes=64)
@@ -158,7 +161,7 @@ def tile_picked_highway_relu_po_kernel(tc, x_words, x_scales, res, w1, w2, offs,
             for first in range(0, SPAN, width):
                 tokens = slice(h * SPAN + first, h * SPAN + first + width)
                 engine.tensor_tensor(
-                    result[h][:, planes, first : first + width], gated[:, planes, tokens], carried[:, planes, tokens], ALU.subtract
+                    result[h][:, planes, first : first + width], gated[:, planes, tokens], carried[:, planes, tokens], ALU.add
                 )
             nc.sync.dma_start(out_rows[:, planes, h * SPAN : (h + 1) * SPAN], result[h][:, planes, :])
 

@@ -18,10 +18,10 @@ ACT = mybir.ActivationFunctionType
 P = 128
 PACK = 4
 HALF = N // 2
+W2_PIECES = ((0, 64, 64), (64, 90, 128))
+W1_PIECES = ((0, 34, 96), (96, 106, 128))
 SPAN = S // 2
-SCALAR_SHARE = 160
-SPLIT = 40
-ROOM = PACK * HALF
+LAST_SCALAR = 160
 
 
 def tile_picked_highway_relu_po_kernel(tc, x_words, x_scales, res, w1, w2, offs, out_0, out_1, out_2):
@@ -39,10 +39,13 @@ def tile_picked_highway_relu_po_kernel(tc, x_words, x_scales, res, w1, w2, offs,
         nc.vector.memset(warm_in[:], 0.0)
         nc.scalar.activation(warm_out[:], warm_in[:], ACT.Sigmoid)
 
-        def load_weight_half(w, room, h):
-            raw = room.rearrange("p (j c) -> p j c", j=PACK)
-            nc.sync.dma_start(raw, w.rearrange("(p j) c -> p j c", j=PACK)[:, :, h * HALF : (h + 1) * HALF])
-            return raw
+        def load_weight(w, name, pieces):
+            raws = []
+            for h, (lo, mid, hi) in enumerate(pieces):
+                raw = pool.tile([P, PACK, PACK * (hi - lo)], F32, name="%s_raw%d" % (name, h), tag="%s_raw%d" % (name, h))
+                nc.sync.dma_start(raw[:], w.rearrange("(p j) c -> p j c", j=PACK)[:, :, PACK * lo : PACK * hi])
+                raws.append(raw)
+            return raws
 
         def load_res(t):
             window = pool.tile([P, T], F32, name="res_window%d" % t)
@@ -55,120 +58,91 @@ def tile_picked_highway_relu_po_kernel(tc, x_words, x_scales, res, w1, w2, offs,
         for q in range(4):
             rows = x_scales[0, 4 * q : 4 * q + 4, :].bitcast(I32)
             nc.sync.dma_start(scale_window[32 * q : 32 * q + 4, :].bitcast(I32), rows)
-        w2_rooms = [pool.tile([P, ROOM], F32, name="w2_room%d" % h) for h in range(2)]
-        w2_raw = [load_weight_half(w2, w2_rooms[h][:], h) for h in range(2)]
-        w1_rooms = [pool.tile([P, ROOM], F32, name="w1_room%d" % h, tag="w1_room%d" % h) for h in range(2)]
-        res_window = [load_res(t) for t in range(2)]
-        w1_raw = [load_weight_half(w1, w1_rooms[0][:], 0)]
-        res_window.append(load_res(2))
-        w1_raw.append(load_weight_half(w1, w1_rooms[1][:], 1))
-        res_window.append(load_res(3))
+        w2_raw = load_weight(w2, "w2", W2_PIECES)
+        w1_raw = load_weight(w1, "w1", W1_PIECES)
+        res_window = [load_res(t) for t in range(PACK)]
 
-        def deal(copy, grouped, raw, h, lo=0, hi=HALF // PACK):
+        def deal(copy, grouped, raw, first, lo, hi):
             dealt = grouped[:].rearrange("p (t m j) -> p m j t", t=PACK, j=PACK)
-            first = h * HALF // PACK
-            copy(dealt[:, first + lo : first + hi], raw.rearrange("p j (m t) -> p m j t", t=PACK)[:, lo:hi])
+            copy(dealt[:, lo:hi], raw[:].rearrange("p j (m t) -> p m j t", t=PACK)[:, lo - first : hi - first])
 
-        def quantise_weight(grouped, name, pieces):
+        def weight_tiles(name):
+            grouped = pool.tile([P, N * PACK], BF16, name=name + "_grouped", align_bytes=64)
             codes = pool.tile([P, N], U32, name=name + "_codes", align_bytes=64)
             scales = pool.tile([P, N], U8, name=name + "_scales", align_bytes=64)
-            width = N // pieces
-            for first in range(0, N, width):
-                cols = slice(first, first + width)
-                nc.vector.quantize_mx(codes[:, cols].bitcast(FP8X4), scales[:, cols], grouped[:, first * PACK : (first + width) * PACK])
-            return codes, scales
+            return grouped, codes, scales
+
+        def quantise_columns(grouped, codes, scales, first, width):
+            cols = slice(first, first + width)
+            nc.vector.quantize_mx(codes[:, cols].bitcast(FP8X4), scales[:, cols], grouped[:, first * PACK : (first + width) * PACK])
 
         x_code = pool.tile([P, S], U32, name="x_code", align_bytes=64)
         nc.vector.tensor_copy(x_code[:], word_window[:].indirect(offsets[:]))
         x_scale = pool.tile([P, S], U8, name="x_scale", align_bytes=64)
         nc.vector.tensor_copy(x_scale[:], scale_window[:].indirect(offsets[:]))
 
-        w2_grouped = pool.tile([P, N * PACK], BF16, name="w2_grouped", align_bytes=64)
-        deal(nc.scalar.copy, w2_grouped, w2_raw[0], 0)
-        deal(nc.vector.tensor_copy, w2_grouped, w2_raw[1], 1)
-        w2_codes, w2_scales = quantise_weight(w2_grouped, "w2", 2)
-
-        gate_banks = []
-        shut = []
-        for t in range(PACK):
+        def product(codes, scales, t, name):
             cols = slice(t * P, (t + 1) * P)
-            bank = psum.tile([P, S], F32, name="gate_bank%d" % t)
+            bank = psum.tile([P, S], F32, name="%s_bank%d" % (name, t))
             nc.tensor.matmul_mx(
                 bank[:],
-                lhsT=w2_codes[:, cols].bitcast(FP8X4),
-                lhsT_scale=w2_scales[:, cols],
+                lhsT=codes[:, cols].bitcast(FP8X4),
+                lhsT_scale=scales[:, cols],
                 rhs=x_code[:].bitcast(FP8X4),
                 rhs_scale=x_scale[:],
                 start=True,
                 stop=True,
             )
-            gate_banks.append(bank)
+            return bank
 
-        for t in range(PACK - 1):
-            closed = pool.tile([P, S], F32, name="shut%d" % t)
-            nc.scalar.activation(closed[:], gate_banks[t][:], ACT.Sigmoid, scale=-1.0)
-            shut.append(closed)
+        def prepare_weight(name, raw, shares):
+            grouped, codes, scales = weight_tiles(name)
+            for piece, (lo, mid, hi) in zip(raw, shares):
+                deal(nc.scalar.copy, grouped, piece, lo, lo, mid)
+                if mid < hi:
+                    deal(nc.vector.tensor_copy, grouped, piece, lo, mid, hi)
+            for first in range(0, N, HALF):
+                quantise_columns(grouped, codes, scales, first, HALF)
+            return [product(codes, scales, t, name) for t in range(PACK)]
 
-        carried = pool.tile([P, PACK, S], F32, name="carried")
+        gate_banks = prepare_weight("w2", w2_raw, W2_PIECES)
+        layer_banks = prepare_weight("w1", w1_raw, W1_PIECES)
 
-        def gather_res(t, tag):
-            picked = pool.tile([P, S], F32, name="passed%d" % t, tag=tag, align_bytes=64)
-            nc.vector.tensor_copy(picked[:], res_window[t][:].indirect(offsets[:]))
-            return picked
-
-        first_passed = gather_res(0, "passed0")
-        nc.vector.tensor_tensor(carried[:, 0, :], first_passed[:], shut[0][:], ALU.mult)
-        for t in (1, 2):
-            nc.vector.tensor_tensor(carried[:, t, :], res_window[t][:].indirect(offsets[:]), shut[t][:], ALU.mult)
-
-        w1_grouped = pool.tile([P, N * PACK], BF16, name="w1_grouped", tag="w1_grouped", align_bytes=64)
-        deal(nc.scalar.copy, w1_grouped, w1_raw[0], 0)
-        deal(nc.scalar.copy, w1_grouped, w1_raw[1], 1, 0, SPLIT)
-        deal(nc.vector.tensor_copy, w1_grouped, w1_raw[1], 1, SPLIT, HALF // PACK)
-        w1_codes, w1_scales = quantise_weight(w1_grouped, "w1", 1)
-        gate = pool.tile([P, PACK + 1, S], F32, name="gate", tag="w1_room1")
-        nc.scalar.activation(gate[:, PACK, :], gate_banks[PACK - 1][:], ACT.Sigmoid, scale=-1.0)
+        gates = pool.tile([P, 2 * PACK, S], F32, name="gates", tag="w1_raw1")
+        shut = gates[:, 0:PACK, :]
+        gate = gates[:, PACK : 2 * PACK, :]
+        nc.scalar.activation(shut[:, 0, :], gate_banks[0][:], ACT.Sigmoid, scale=-1.0)
         for t in range(PACK):
             nc.scalar.activation(gate[:, t, :], gate_banks[t][:], ACT.Sigmoid)
-        last_passed = gather_res(3, "w1_grouped")
-        nc.gpsimd.tensor_tensor(carried[:, 3, :], last_passed[:], gate[:, PACK, :], ALU.mult)
+        for h in range(2):
+            for t in range(1, PACK):
+                tokens = slice(h * SPAN, (h + 1) * SPAN)
+                nc.scalar.activation(shut[:, t, tokens], gate_banks[t][:, tokens], ACT.Sigmoid, scale=-1.0)
 
+        carried = pool.tile([P, PACK, S], F32, name="carried")
+        gated = pool.tile([P, PACK, S], F32, name="gated")
+        result = pool.tile([P, PACK, S], F32, name="result")
         out_codes = pool.tile([P, S], U32, name="out_codes", align_bytes=64)
         out_scales = pool.tile([P, S], U8, name="out_scales", align_bytes=64)
         out_rows = out_0.rearrange("(p t) s -> p t s", t=PACK)
         out_words = out_1[0].rearrange("p s r -> p (s r)").bitcast(I32)
 
-        gated = pool.tile([P, PACK, S], F32, name="gated")
-        for t in range(PACK):
-            cols = slice(t * P, (t + 1) * P)
-            bank = psum.tile([P, S], F32, name="layer_bank%d" % t)
-            nc.tensor.matmul_mx(
-                bank[:],
-                lhsT=w1_codes[:, cols].bitcast(FP8X4),
-                lhsT_scale=w1_scales[:, cols],
-                rhs=x_code[:].bitcast(FP8X4),
-                rhs_scale=x_scale[:],
-                start=True,
-                stop=True,
-            )
-            nc.vector.scalar_tensor_tensor(gated[:, t, :], bank[:], 0.0, gate[:, t, :], ALU.max, ALU.mult)
+        def carry(t, closed, lo, hi):
+            picked = res_window[t][:].indirect(offsets[:, lo // 16 : hi // 16])
+            nc.vector.tensor_tensor(carried[:, t, lo:hi], picked, closed[:, lo:hi], ALU.mult)
 
-        result = [pool.tile([P, PACK, SPAN], F32, name="result%d" % h) for h in range(2)]
+        def combine(engine, planes, lo, hi):
+            engine.tensor_tensor(result[:, planes, lo:hi], gated[:, planes, lo:hi], carried[:, planes, lo:hi], ALU.add)
+
+        def store(planes, lo, hi):
+            nc.sync.dma_start(out_rows[:, planes, lo:hi], result[:, planes, lo:hi])
+
         grouped = [pool.tile([P, SPAN, PACK], BF16, name="out_grouped%d" % h, align_bytes=64) for h in range(2)]
 
-        def combine(engine, planes, h, pieces):
-            width = SPAN // pieces
-            for first in range(0, SPAN, width):
-                tokens = slice(h * SPAN + first, h * SPAN + first + width)
-                engine.tensor_tensor(
-                    result[h][:, planes, first : first + width], gated[:, planes, tokens], carried[:, planes, tokens], ALU.add
-                )
-            nc.sync.dma_start(out_rows[:, planes, h * SPAN : (h + 1) * SPAN], result[h][:, planes, :])
-
-        def interleave(copy, h, part):
+        def interleave(copy, h, lo, hi):
             copy(
-                grouped[h][:, part, :].rearrange("p (c i) t -> p c t i", i=4),
-                result[h][:, :, part].rearrange("p t (c i) -> p c t i", i=4),
+                grouped[h][:, lo:hi, :].rearrange("p (c i) t -> p c t i", i=4),
+                result[:, :, h * SPAN + lo : h * SPAN + hi].rearrange("p t (c i) -> p c t i", i=4),
             )
 
         def quantise_out(h):
@@ -176,15 +150,27 @@ def tile_picked_highway_relu_po_kernel(tc, x_words, x_scales, res, w1, w2, offs,
             nc.vector.quantize_mx(out_codes[:, tokens].bitcast(FP8X4), out_scales[:, tokens], grouped[h][:].rearrange("p s t -> p (s t)"))
             nc.sync.dma_start(out_words[:, tokens], out_codes[:, tokens].bitcast(I32))
 
-        for h in range(2):
-            combine(nc.gpsimd, slice(0, 1), h, 1)
-        combine(nc.vector, slice(1, PACK), 0, 2)
-        combine(nc.vector, slice(1, PACK), 1, 1)
-        interleave(nc.scalar.copy, 0, slice(0, SPAN // 2))
-        interleave(nc.scalar.copy, 0, slice(SPAN // 2, SPAN))
-        interleave(nc.scalar.copy, 1, slice(0, SCALAR_SHARE))
+        carry(0, shut[:, 0, :], 0, S)
+        for t in range(PACK):
+            nc.vector.scalar_tensor_tensor(gated[:, t, :], layer_banks[t][:], 0.0, gate[:, t, :], ALU.max, ALU.mult)
+        combine(nc.gpsimd, slice(0, 1), 0, S)
+        store(slice(0, 1), 0, S)
+        later = slice(1, PACK)
+        for t in range(1, PACK):
+            carry(t, shut[:, t, :], 0, SPAN)
+        combine(nc.vector, later, 0, SPAN)
+        store(later, 0, SPAN)
+        interleave(nc.scalar.copy, 0, 0, SPAN)
+        for t in range(1, PACK):
+            carry(t, shut[:, t, :], SPAN, S)
         quantise_out(0)
-        interleave(nc.vector.tensor_copy, 1, slice(SCALAR_SHARE, SPAN))
+        middle = SPAN + SPAN // 2
+        combine(nc.vector, later, SPAN, middle)
+        combine(nc.vector, later, middle, S)
+        store(later, SPAN, S)
+        interleave(nc.scalar.copy, 1, 0, SPAN // 2)
+        interleave(nc.scalar.copy, 1, SPAN // 2, LAST_SCALAR)
+        interleave(nc.vector.tensor_copy, 1, LAST_SCALAR, SPAN)
         quantise_out(1)
         for q in range(4):
             queue = nc.scalar if q % 2 else nc.sync

@@ -1,6 +1,7 @@
 from contextlib import ExitStack
 
 import concourse.mybir as mybir
+from concourse.masks import make_identity
 
 K, T, S, N = 512, 1024, 512, 512
 FLOPS = 2 * 2 * K * N * S
@@ -21,7 +22,7 @@ HALF = N // 2
 W2_PIECES = ((0, 64, 64), (64, 90, 128))
 W1_PIECES = ((0, 34, 96), (96, 106, 128))
 SPAN = S // 2
-LAST_SCALAR = 160
+SCALAR_TOKENS = (160, 64)
 
 
 def tile_picked_highway_relu_po_kernel(tc, x_words, x_scales, res, w1, w2, offs, out_0, out_1, out_2):
@@ -38,6 +39,9 @@ def tile_picked_highway_relu_po_kernel(tc, x_words, x_scales, res, w1, w2, offs,
         warm_out = pool.tile([P, 1], F32, name="warm_out")
         nc.vector.memset(warm_in[:], 0.0)
         nc.scalar.activation(warm_out[:], warm_in[:], ACT.Sigmoid)
+
+        identity = pool.tile([P, P], F32, name="identity")
+        make_identity(nc, identity[:])
 
         def load_weight(w, name, pieces):
             raws = []
@@ -83,7 +87,7 @@ def tile_picked_highway_relu_po_kernel(tc, x_words, x_scales, res, w1, w2, offs,
 
         def product(codes, scales, t, name):
             cols = slice(t * P, (t + 1) * P)
-            bank = psum.tile([P, S], F32, name="%s_bank%d" % (name, t))
+            bank = psum.tile([P, S], F32, name="%s_bank%d" % (name, t), tag="%s_bank%d" % (name, t))
             nc.tensor.matmul_mx(
                 bank[:],
                 lhsT=codes[:, cols].bitcast(FP8X4),
@@ -111,13 +115,12 @@ def tile_picked_highway_relu_po_kernel(tc, x_words, x_scales, res, w1, w2, offs,
         gates = pool.tile([P, 2 * PACK, S], F32, name="gates", tag="w1_raw1")
         shut = gates[:, 0:PACK, :]
         gate = gates[:, PACK : 2 * PACK, :]
-        nc.scalar.activation(shut[:, 0, :], gate_banks[0][:], ACT.Sigmoid, scale=-1.0)
+        for t in (0, 1):
+            nc.scalar.activation(shut[:, t, :], gate_banks[t][:], ACT.Sigmoid, scale=-1.0)
         for t in range(PACK):
             nc.scalar.activation(gate[:, t, :], gate_banks[t][:], ACT.Sigmoid)
-        for h in range(2):
-            for t in range(1, PACK):
-                tokens = slice(h * SPAN, (h + 1) * SPAN)
-                nc.scalar.activation(shut[:, t, tokens], gate_banks[t][:, tokens], ACT.Sigmoid, scale=-1.0)
+        for t in (2, 3):
+            nc.scalar.activation(shut[:, t, :], gate_banks[t][:], ACT.Sigmoid, scale=-1.0)
 
         carried = pool.tile([P, PACK, S], F32, name="carried")
         gated = pool.tile([P, PACK, S], F32, name="gated")
@@ -150,28 +153,41 @@ def tile_picked_highway_relu_po_kernel(tc, x_words, x_scales, res, w1, w2, offs,
             nc.vector.quantize_mx(out_codes[:, tokens].bitcast(FP8X4), out_scales[:, tokens], grouped[h][:].rearrange("p s t -> p (s t)"))
             nc.sync.dma_start(out_words[:, tokens], out_codes[:, tokens].bitcast(I32))
 
-        carry(0, shut[:, 0, :], 0, S)
+        def combine_by_transposes(t, h):
+            blocks = SPAN // P
+            turned_bank = psum.tile([P, blocks, P], F32, name="turned_bank%d" % h, tag="w2_bank%d" % (2 + h))
+            for k in range(blocks):
+                tokens = slice(h * SPAN + k * P, h * SPAN + (k + 1) * P)
+                nc.tensor.matmul(turned_bank[:, k, :], carried[:, t, tokens], identity[:], start=True, stop=False, is_transpose=True)
+                nc.tensor.matmul(turned_bank[:, k, :], gated[:, t, tokens], identity[:], start=False, stop=True, is_transpose=True)
+            turned = pool.tile([P, blocks, P], F32, name="turned%d" % h)
+            nc.scalar.copy(turned[:], turned_bank[:])
+            back_bank = psum.tile([P, blocks, P], F32, name="back_bank%d" % h, tag="w1_bank%d" % h)
+            for k in range(blocks):
+                nc.tensor.transpose(back_bank[:, k, :], turned[:, k, :], identity[:])
+            nc.scalar.copy(result[:, t, h * SPAN : (h + 1) * SPAN], back_bank[:].rearrange("p k c -> p (k c)"))
+
+        for t in (0, 1):
+            carry(t, shut[:, t, :], 0, S)
         for t in range(PACK):
             nc.vector.scalar_tensor_tensor(gated[:, t, :], layer_banks[t][:], 0.0, gate[:, t, :], ALU.max, ALU.mult)
         combine(nc.gpsimd, slice(0, 1), 0, S)
         store(slice(0, 1), 0, S)
-        later = slice(1, PACK)
-        for t in range(1, PACK):
-            carry(t, shut[:, t, :], 0, SPAN)
-        combine(nc.vector, later, 0, SPAN)
-        store(later, 0, SPAN)
-        interleave(nc.scalar.copy, 0, 0, SPAN)
-        for t in range(1, PACK):
-            carry(t, shut[:, t, :], SPAN, S)
-        quantise_out(0)
-        middle = SPAN + SPAN // 2
-        combine(nc.vector, later, SPAN, middle)
-        combine(nc.vector, later, middle, S)
-        store(later, SPAN, S)
-        interleave(nc.scalar.copy, 1, 0, SPAN // 2)
-        interleave(nc.scalar.copy, 1, SPAN // 2, LAST_SCALAR)
-        interleave(nc.vector.tensor_copy, 1, LAST_SCALAR, SPAN)
-        quantise_out(1)
+        for h in range(2):
+            combine_by_transposes(1, h)
+        store(slice(1, 2), 0, S)
+        later = slice(2, PACK)
+        carry(2, shut[:, 2, :], 0, S)
+        for h in range(2):
+            carry(3, shut[:, 3, :], h * SPAN, (h + 1) * SPAN)
+        for h in range(2):
+            combine(nc.vector, later, h * SPAN, (h + 1) * SPAN)
+            store(later, h * SPAN, (h + 1) * SPAN)
+        for h in range(2):
+            interleave(nc.scalar.copy, h, 0, SCALAR_TOKENS[h])
+            interleave(nc.vector.tensor_copy, h, SCALAR_TOKENS[h], SPAN)
+        for h in range(2):
+            quantise_out(h)
         for q in range(4):
             queue = nc.scalar if q % 2 else nc.sync
             queue.dma_start(out_2[0, 4 * q : 4 * q + 4, :].bitcast(I32), out_scales[32 * q : 32 * q + 4, :].bitcast(I32))

@@ -112,15 +112,23 @@ def tile_picked_highway_relu_po_kernel(tc, x_words, x_scales, res, w1, w2, offs,
         gate_banks = prepare_weight("w2", w2_raw, W2_PIECES)
         layer_banks = prepare_weight("w1", w1_raw, W1_PIECES)
 
-        gates = pool.tile([P, 2 * PACK, S], F32, name="gates", tag="w1_raw1")
+        gates = pool.tile([P, 2 * PACK, S], F32, name="gates", tag="w1_raw0")
         shut = gates[:, 0:PACK, :]
         gate = gates[:, PACK : 2 * PACK, :]
-        for t in (0, 1):
+
+        def close_gate(t):
             nc.scalar.activation(shut[:, t, :], gate_banks[t][:], ACT.Sigmoid, scale=-1.0)
-        for t in range(PACK):
+
+        def open_gate(t):
             nc.scalar.activation(gate[:, t, :], gate_banks[t][:], ACT.Sigmoid)
-        for t in (2, 3):
-            nc.scalar.activation(shut[:, t, :], gate_banks[t][:], ACT.Sigmoid, scale=-1.0)
+
+        close_gate(0)
+        close_gate(1)
+        open_gate(0)
+        close_gate(3)
+        for t in (1, 2, 3):
+            open_gate(t)
+        close_gate(2)
 
         carried = pool.tile([P, PACK, S], F32, name="carried")
         gated = pool.tile([P, PACK, S], F32, name="gated")
@@ -155,27 +163,31 @@ def tile_picked_highway_relu_po_kernel(tc, x_words, x_scales, res, w1, w2, offs,
 
         def combine_by_transposes(t, h):
             blocks = SPAN // P
-            turned_bank = psum.tile([P, blocks, P], F32, name="turned_bank%d" % h, tag="w2_bank%d" % (2 + h))
+            turned_bank = psum.tile([P, blocks, P], F32, name="turned_bank%d" % h, tag=("w2_bank0", "w1_bank0")[h])
             for k in range(blocks):
                 tokens = slice(h * SPAN + k * P, h * SPAN + (k + 1) * P)
                 nc.tensor.matmul(turned_bank[:, k, :], carried[:, t, tokens], identity[:], start=True, stop=False, is_transpose=True)
                 nc.tensor.matmul(turned_bank[:, k, :], gated[:, t, tokens], identity[:], start=False, stop=True, is_transpose=True)
             turned = pool.tile([P, blocks, P], F32, name="turned%d" % h)
             nc.scalar.copy(turned[:], turned_bank[:])
-            back_bank = psum.tile([P, blocks, P], F32, name="back_bank%d" % h, tag="w1_bank%d" % h)
+            back_bank = psum.tile([P, blocks, P], F32, name="back_bank%d" % h, tag=("w2_bank1", "w1_bank1")[h])
             for k in range(blocks):
                 nc.tensor.transpose(back_bank[:, k, :], turned[:, k, :], identity[:])
             nc.scalar.copy(result[:, t, h * SPAN : (h + 1) * SPAN], back_bank[:].rearrange("p k c -> p (k c)"))
 
-        for t in (0, 1):
-            carry(t, shut[:, t, :], 0, S)
-        for t in range(PACK):
+        def rectify(t):
             nc.vector.scalar_tensor_tensor(gated[:, t, :], layer_banks[t][:], 0.0, gate[:, t, :], ALU.max, ALU.mult)
-        combine(nc.gpsimd, slice(0, 1), 0, S)
-        store(slice(0, 1), 0, S)
-        for h in range(2):
-            combine_by_transposes(1, h)
+
+        carry(0, shut[:, 0, :], 0, S)
+        rectify(0)
+        carry(1, shut[:, 1, :], 0, S)
+        for t in (1, 2, 3):
+            rectify(t)
+        combine(nc.gpsimd, slice(1, 2), 0, S)
         store(slice(1, 2), 0, S)
+        for h in range(2):
+            combine_by_transposes(0, h)
+        store(slice(0, 1), 0, S)
         later = slice(2, PACK)
         carry(2, shut[:, 2, :], 0, S)
         for h in range(2):

@@ -161,16 +161,16 @@ def tile_picked_highway_relu_po_kernel(tc, x_words, x_scales, res, w1, w2, offs,
             nc.vector.quantize_mx(out_codes[:, tokens].bitcast(FP8X4), out_scales[:, tokens], grouped[h][:].rearrange("p s t -> p (s t)"))
             nc.sync.dma_start(out_words[:, tokens], out_codes[:, tokens].bitcast(I32))
 
-        def combine_by_transposes(t, h):
+        def combine_by_transposes(t, h, turned_tag, back_tag):
             blocks = SPAN // P
-            turned_bank = psum.tile([P, blocks, P], F32, name="turned_bank%d" % h, tag=("w2_bank0", "w1_bank0")[h])
+            turned_bank = psum.tile([P, blocks, P], F32, name="turned_bank%d%d" % (t, h), tag=turned_tag)
             for k in range(blocks):
                 tokens = slice(h * SPAN + k * P, h * SPAN + (k + 1) * P)
                 nc.tensor.matmul(turned_bank[:, k, :], carried[:, t, tokens], identity[:], start=True, stop=False, is_transpose=True)
                 nc.tensor.matmul(turned_bank[:, k, :], gated[:, t, tokens], identity[:], start=False, stop=True, is_transpose=True)
-            turned = pool.tile([P, blocks, P], F32, name="turned%d" % h)
+            turned = pool.tile([P, blocks, P], F32, name="turned%d%d" % (t, h))
             nc.scalar.copy(turned[:], turned_bank[:])
-            back_bank = psum.tile([P, blocks, P], F32, name="back_bank%d" % h, tag=("w2_bank1", "w1_bank1")[h])
+            back_bank = psum.tile([P, blocks, P], F32, name="back_bank%d%d" % (t, h), tag=back_tag)
             for k in range(blocks):
                 nc.tensor.transpose(back_bank[:, k, :], turned[:, k, :], identity[:])
             nc.scalar.copy(result[:, t, h * SPAN : (h + 1) * SPAN], back_bank[:].rearrange("p k c -> p (k c)"))
@@ -183,11 +183,12 @@ def tile_picked_highway_relu_po_kernel(tc, x_words, x_scales, res, w1, w2, offs,
         carry(1, shut[:, 1, :], 0, S)
         for t in (1, 2, 3):
             rectify(t)
-        combine(nc.gpsimd, slice(1, 2), 0, S)
-        store(slice(1, 2), 0, S)
-        for h in range(2):
-            combine_by_transposes(0, h)
+        combine(nc.gpsimd, slice(1, 2), 0, SPAN)
+        combine_by_transposes(0, 0, "w2_bank0", "w2_bank1")
+        combine_by_transposes(0, 1, "w1_bank0", "w1_bank1")
         store(slice(0, 1), 0, S)
+        combine_by_transposes(1, 1, "w2_bank3", "w2_bank2")
+        store(slice(1, 2), 0, S)
         later = slice(2, PACK)
         carry(2, shut[:, 2, :], 0, S)
         for h in range(2):

@@ -85,53 +85,69 @@ def tile_picked_highway_relu_po_kernel(tc, x_words, x_scales, res, w1, w2, offs,
         x_scale = pool.tile([P, S], U8, name="x_scale", align_bytes=64)
         nc.vector.tensor_copy(x_scale[:], scale_window[:].indirect(offsets[:]))
 
-        def product(codes, scales, t, name):
-            cols = slice(t * P, (t + 1) * P)
-            bank = psum.tile([P, S], F32, name="%s_bank%d" % (name, t), tag="%s_bank%d" % (name, t))
+        def multiply(out, stationary, moving):
             nc.tensor.matmul_mx(
-                bank[:],
-                lhsT=codes[:, cols].bitcast(FP8X4),
-                lhsT_scale=scales[:, cols],
-                rhs=x_code[:].bitcast(FP8X4),
-                rhs_scale=x_scale[:],
+                out,
+                lhsT=stationary[0].bitcast(FP8X4),
+                lhsT_scale=stationary[1],
+                rhs=moving[0].bitcast(FP8X4),
+                rhs_scale=moving[1],
                 start=True,
                 stop=True,
             )
+
+        def by_features(weight, t, tag):
+            bank = psum.tile([P, S], F32, name="features_" + tag, tag=tag)
+            cols = slice(t * P, (t + 1) * P)
+            multiply(bank[:], (weight[0][:, cols], weight[1][:, cols]), (x_code[:], x_scale[:]))
             return bank
 
-        def prepare_weight(name, raw, shares):
+        def by_tokens(weight, h, tag):
+            bank = psum.tile([P, 2, HALF], F32, name="tokens_" + tag, tag=tag)
+            for k in range(2):
+                tokens = slice(h * SPAN + k * P, h * SPAN + (k + 1) * P)
+                multiply(bank[:, k, :], (x_code[:, tokens], x_scale[:, tokens]), (weight[0][:, 0:HALF], weight[1][:, 0:HALF]))
+            return bank
+
+        def prepare_weight(name, raw, shares, firsts):
             grouped, codes, scales = weight_tiles(name)
             for piece, (lo, mid, hi) in zip(raw, shares):
                 deal(nc.scalar.copy, grouped, piece, lo, lo, mid)
                 if mid < hi:
                     deal(nc.vector.tensor_copy, grouped, piece, lo, mid, hi)
-            for first in range(0, N, HALF):
+            for first in firsts:
                 quantise_columns(grouped, codes, scales, first, HALF)
-            return [product(codes, scales, t, name) for t in range(PACK)]
+            return codes, scales
 
-        gate_banks = prepare_weight("w2", w2_raw, W2_PIECES)
-        layer_banks = prepare_weight("w1", w1_raw, W1_PIECES)
+        w2_mx = prepare_weight("w2", w2_raw, W2_PIECES, (0, HALF))
+        gate_banks = [by_features(w2_mx, t, "bank%d" % t) for t in range(3)]
+        gate_turned_banks = [by_tokens(w2_mx, h, "bank%d" % (4 + h)) for h in range(2)]
+        gate_banks.append(by_features(w2_mx, 3, "bank3"))
+        w1_mx = prepare_weight("w1", w1_raw, W1_PIECES, (HALF, 0))
+        layer_banks = {2: by_features(w1_mx, 2, "bank6")}
 
         gates = pool.tile([P, 2 * PACK, S], F32, name="gates", tag="w1_raw0")
         shut = gates[:, 0:PACK, :]
-        gate = gates[:, PACK : 2 * PACK, :]
+        gate_turned = gates[:, PACK : PACK + 2, :]
+        gate = {2: gates[:, PACK + 2, :], 3: gates[:, PACK + 3, :]}
+        shut_half = pool.tile([P, SPAN], F32, name="shut_half", tag="w1_raw1")
 
-        def close_gate(t):
-            nc.scalar.activation(shut[:, t, :], gate_banks[t][:], ACT.Sigmoid, scale=-1.0)
+        def close_gate(target, t, lo, hi):
+            nc.scalar.activation(target, gate_banks[t][:, lo:hi], ACT.Sigmoid, scale=-1.0)
 
-        def open_gate(t):
-            nc.scalar.activation(gate[:, t, :], gate_banks[t][:], ACT.Sigmoid)
+        def open_gate(target, bank):
+            nc.scalar.activation(target, bank, ACT.Sigmoid)
 
-        close_gate(0)
-        close_gate(1)
-        open_gate(0)
-        close_gate(3)
-        for t in (1, 2, 3):
-            open_gate(t)
-        close_gate(2)
+        for t in (0, 1):
+            close_gate(shut[:, t, :], t, 0, S)
+        layer_turned_banks = [by_tokens(w1_mx, h, "bank%d" % h) for h in range(2)]
+        layer_banks[3] = by_features(w1_mx, 3, "bank7")
+        close_gate(shut_half[:], 2, 0, SPAN)
+        close_gate(shut[:, 2, SPAN:S], 2, SPAN, S)
+        open_gate(gate_turned[:, 0, :], gate_turned_banks[0][:].rearrange("p k c -> p (k c)"))
+        open_gate(gate[2], gate_banks[2][:])
 
         carried = pool.tile([P, PACK, S], F32, name="carried")
-        gated = pool.tile([P, PACK, S], F32, name="gated")
         result = pool.tile([P, PACK, S], F32, name="result")
         out_codes = pool.tile([P, S], U32, name="out_codes", align_bytes=64)
         out_scales = pool.tile([P, S], U8, name="out_scales", align_bytes=64)
@@ -140,10 +156,7 @@ def tile_picked_highway_relu_po_kernel(tc, x_words, x_scales, res, w1, w2, offs,
 
         def carry(t, closed, lo, hi):
             picked = res_window[t][:].indirect(offsets[:, lo // 16 : hi // 16])
-            nc.vector.tensor_tensor(carried[:, t, lo:hi], picked, closed[:, lo:hi], ALU.mult)
-
-        def combine(engine, planes, lo, hi):
-            engine.tensor_tensor(result[:, planes, lo:hi], gated[:, planes, lo:hi], carried[:, planes, lo:hi], ALU.add)
+            nc.vector.tensor_tensor(carried[:, t, lo:hi], picked, closed, ALU.mult)
 
         def store(planes, lo, hi):
             nc.sync.dma_start(out_rows[:, planes, lo:hi], result[:, planes, lo:hi])
@@ -161,41 +174,55 @@ def tile_picked_highway_relu_po_kernel(tc, x_words, x_scales, res, w1, w2, offs,
             nc.vector.quantize_mx(out_codes[:, tokens].bitcast(FP8X4), out_scales[:, tokens], grouped[h][:].rearrange("p s t -> p (s t)"))
             nc.sync.dma_start(out_words[:, tokens], out_codes[:, tokens].bitcast(I32))
 
-        def combine_by_transposes(t, h, turned_tag, back_tag):
-            blocks = SPAN // P
-            turned_bank = psum.tile([P, blocks, P], F32, name="turned_bank%d%d" % (t, h), tag=turned_tag)
-            for k in range(blocks):
-                tokens = slice(h * SPAN + k * P, h * SPAN + (k + 1) * P)
-                nc.tensor.matmul(turned_bank[:, k, :], carried[:, t, tokens], identity[:], start=True, stop=False, is_transpose=True)
-                nc.tensor.matmul(turned_bank[:, k, :], gated[:, t, tokens], identity[:], start=False, stop=True, is_transpose=True)
-            turned = pool.tile([P, blocks, P], F32, name="turned%d%d" % (t, h))
-            nc.scalar.copy(turned[:], turned_bank[:])
-            back_bank = psum.tile([P, blocks, P], F32, name="back_bank%d%d" % (t, h), tag=back_tag)
-            for k in range(blocks):
-                nc.tensor.transpose(back_bank[:, k, :], turned[:, k, :], identity[:])
-            nc.scalar.copy(result[:, t, h * SPAN : (h + 1) * SPAN], back_bank[:].rearrange("p k c -> p (k c)"))
+        blocks = S // P
+        carried_turned = pool.tile([P, 2, blocks, P], F32, name="carried_turned")
 
-        def rectify(t):
-            nc.vector.scalar_tensor_tensor(gated[:, t, :], layer_banks[t][:], 0.0, gate[:, t, :], ALU.max, ALU.mult)
+        def turn_carried(t, tag):
+            bank = psum.tile([P, blocks, P], F32, name="carried_bank%d" % t, tag=tag)
+            for k in range(blocks):
+                nc.tensor.transpose(bank[:, k, :], carried[:, t, k * P : (k + 1) * P], identity[:])
+            nc.scalar.copy(carried_turned[:, t], bank[:])
 
         carry(0, shut[:, 0, :], 0, S)
-        rectify(0)
+        turn_carried(0, "bank4")
+        open_gate(gate_turned[:, 1, :], gate_turned_banks[1][:].rearrange("p k c -> p (k c)"))
         carry(1, shut[:, 1, :], 0, S)
-        for t in (1, 2, 3):
-            rectify(t)
-        combine(nc.gpsimd, slice(1, 2), 0, SPAN)
-        combine_by_transposes(0, 0, "w2_bank0", "w2_bank1")
-        combine_by_transposes(0, 1, "w1_bank0", "w1_bank1")
-        store(slice(0, 1), 0, S)
-        combine_by_transposes(1, 1, "w2_bank3", "w2_bank2")
-        store(slice(1, 2), 0, S)
-        later = slice(2, PACK)
-        carry(2, shut[:, 2, :], 0, S)
+        turn_carried(1, "bank2")
+        open_gate(gate[3], gate_banks[3][:])
+        close_gate(shut[:, 3, :], 3, 0, S)
+        carry(2, shut_half[:], 0, SPAN)
+        carry(2, shut[:, 2, SPAN:S], SPAN, S)
+
+        products = pool.tile([P, PACK, S], F32, name="products", tag="w1_raw1")
+
+        def rectify(slot, bank, opened):
+            nc.vector.scalar_tensor_tensor(products[:, slot, :], bank, 0.0, opened, ALU.max, ALU.mult)
+
+        def add_turned(h, tag):
+            bank = psum.tile([P, 2, 2, P], F32, name="sum_bank%d" % h, tag=tag)
+            turned = products[:, h, :].rearrange("p (k t m) -> p k t m", k=2, t=2)
+            places = [(t, k) for t in range(2) for k in range(2)]
+            for i, (t, k) in enumerate(places):
+                nc.tensor.matmul(bank[:, t, k, :], carried_turned[:, t, 2 * h + k, :], identity[:], start=i == 0, stop=False, is_transpose=True)
+            for i, (t, k) in enumerate(places):
+                nc.tensor.matmul(bank[:, t, k, :], turned[:, k, t, :], identity[:], start=False, stop=i == len(places) - 1, is_transpose=True)
+            nc.scalar.copy(result[:, 0:2, h * SPAN : (h + 1) * SPAN], bank[:].rearrange("p t k c -> p t (k c)"))
+
+        rectify(2, layer_banks[2][:], gate[2])
+        nc.gpsimd.tensor_tensor(result[:, 2, :], products[:, 2, :], carried[:, 2, :], ALU.add)
+        store(2, 0, S)
         for h in range(2):
-            carry(3, shut[:, 3, :], h * SPAN, (h + 1) * SPAN)
+            rectify(h, layer_turned_banks[h][:].rearrange("p k c -> p (k c)"), gate_turned[:, h, :])
+        rectify(3, layer_banks[3][:], gate[3])
         for h in range(2):
-            combine(nc.vector, later, h * SPAN, (h + 1) * SPAN)
-            store(later, h * SPAN, (h + 1) * SPAN)
+            add_turned(h, "bank%d" % (5 - h))
+            store(slice(0, 2), h * SPAN, (h + 1) * SPAN)
+        for h in range(2):
+            carry(3, shut[:, 3, h * SPAN : (h + 1) * SPAN], h * SPAN, (h + 1) * SPAN)
+        for h in range(2):
+            tokens = slice(h * SPAN, (h + 1) * SPAN)
+            nc.vector.tensor_tensor(result[:, 3, tokens], products[:, 3, tokens], carried[:, 3, tokens], ALU.add)
+        store(3, 0, S)
         for h in range(2):
             interleave(nc.scalar.copy, h, 0, SCALAR_TOKENS[h])
             interleave(nc.vector.tensor_copy, h, SCALAR_TOKENS[h], SPAN)

@@ -22,7 +22,7 @@ HALF = N // 2
 W2_PIECES = ((0, 64, 64), (64, 90, 128))
 W1_PIECES = ((0, 34, 96), (96, 106, 128))
 SPAN = S // 2
-SCALAR_TOKENS = (160, 64)
+SCALAR_TOKENS = (128, 48)
 
 
 def tile_picked_highway_relu_po_kernel(tc, x_words, x_scales, res, w1, w2, offs, out_0, out_1, out_2):

@@ -22,7 +22,7 @@ HALF = N // 2
 W2_PIECES = ((0, 64, 64), (64, 90, 128))
 W1_PIECES = ((0, 34, 96), (96, 106, 128))
 SPAN = S // 2
-SCALAR_TOKENS = (128, 48)
+SCALAR_TOKENS = 128
 
 
 def tile_picked_highway_relu_po_kernel(tc, x_words, x_scales, res, w1, w2, offs, out_0, out_1, out_2):
@@ -223,9 +223,9 @@ def tile_picked_highway_relu_po_kernel(tc, x_words, x_scales, res, w1, w2, offs,
             tokens = slice(h * SPAN, (h + 1) * SPAN)
             nc.vector.tensor_tensor(result[:, 3, tokens], products[:, 3, tokens], carried[:, 3, tokens], ALU.add)
         store(3, 0, S)
-        for h in range(2):
-            interleave(nc.scalar.copy, h, 0, SCALAR_TOKENS[h])
-            interleave(nc.vector.tensor_copy, h, SCALAR_TOKENS[h], SPAN)
+        interleave(nc.vector.tensor_copy, 0, 0, SPAN)
+        interleave(nc.scalar.copy, 1, 0, SCALAR_TOKENS)
+        interleave(nc.vector.tensor_copy, 1, SCALAR_TOKENS, SPAN)
         for h in range(2):
             quantise_out(h)
         for q in range(4):

@@ -1,7 +1,6 @@
 from contextlib import ExitStack
 
 import concourse.mybir as mybir
-from concourse.masks import make_identity
 
 K, T, S, N = 512, 1024, 512, 512
 FLOPS = 2 * 2 * K * N * S
@@ -19,10 +18,10 @@ ACT = mybir.ActivationFunctionType
 P = 128
 PACK = 4
 HALF = N // 2
-W2_PIECES = ((0, 64, 64), (64, 90, 128))
-W1_PIECES = ((0, 34, 96), (96, 106, 128))
 SPAN = S // 2
-SCALAR_TOKENS = 128
+W2_PIECES = ((0, 64, 64), (64, 90, 128))
+W1_PIECES = ((0, 0, 64), (64, 64, 96), (96, 96, 128))
+SCALAR_TOKENS = 96
 
 
 def tile_picked_highway_relu_po_kernel(tc, x_words, x_scales, res, w1, w2, offs, out_0, out_1, out_2):
@@ -40,19 +39,16 @@ def tile_picked_highway_relu_po_kernel(tc, x_words, x_scales, res, w1, w2, offs,
         nc.vector.memset(warm_in[:], 0.0)
         nc.scalar.activation(warm_out[:], warm_in[:], ACT.Sigmoid)
 
-        identity = pool.tile([P, P], F32, name="identity")
-        make_identity(nc, identity[:])
-
         def load_weight(w, name, pieces):
             raws = []
             for h, (lo, mid, hi) in enumerate(pieces):
-                raw = pool.tile([P, PACK, PACK * (hi - lo)], F32, name="%s_raw%d" % (name, h), tag="%s_raw%d" % (name, h))
+                raw = pool.tile([P, PACK, PACK * (hi - lo)], F32, name="%s_raw%d" % (name, h))
                 nc.sync.dma_start(raw[:], w.rearrange("(p j) c -> p j c", j=PACK)[:, :, PACK * lo : PACK * hi])
                 raws.append(raw)
             return raws
 
         def load_res(t):
-            window = pool.tile([P, T], F32, name="res_window%d" % t)
+            window = pool.tile([P, T], F32, name="res_window%d" % t, tag="res_window%d" % t)
             nc.sync.dma_start(window[:], res.rearrange("(p t) c -> p t c", t=PACK)[:, t, :])
             return window
 
@@ -66,100 +62,106 @@ def tile_picked_highway_relu_po_kernel(tc, x_words, x_scales, res, w1, w2, offs,
         w1_raw = load_weight(w1, "w1", W1_PIECES)
         res_window = [load_res(t) for t in range(PACK)]
 
-        def deal(copy, grouped, raw, first, lo, hi):
-            dealt = grouped[:].rearrange("p (t m j) -> p m j t", t=PACK, j=PACK)
-            copy(dealt[:, lo:hi], raw[:].rearrange("p j (m t) -> p m j t", t=PACK)[:, lo - first : hi - first])
-
-        def weight_tiles(name):
-            grouped = pool.tile([P, N * PACK], BF16, name=name + "_grouped", align_bytes=64)
-            codes = pool.tile([P, N], U32, name=name + "_codes", align_bytes=64)
-            scales = pool.tile([P, N], U8, name=name + "_scales", align_bytes=64)
-            return grouped, codes, scales
-
-        def quantise_columns(grouped, codes, scales, first, width):
-            cols = slice(first, first + width)
-            nc.vector.quantize_mx(codes[:, cols].bitcast(FP8X4), scales[:, cols], grouped[:, first * PACK : (first + width) * PACK])
-
         x_code = pool.tile([P, S], U32, name="x_code", align_bytes=64)
         nc.vector.tensor_copy(x_code[:], word_window[:].indirect(offsets[:]))
         x_scale = pool.tile([P, S], U8, name="x_scale", align_bytes=64)
         nc.vector.tensor_copy(x_scale[:], scale_window[:].indirect(offsets[:]))
 
-        def multiply(out, stationary, moving):
+        def round_on_scalar(target, source, sign):
+            nc.scalar.activation(target, source, ACT.Copy, scale=sign)
+
+        def round_on_vector(target, source, sign):
+            nc.vector.tensor_scalar(target, source, sign, None, ALU.mult)
+
+        def prepare_weight(name, raw, pieces, sign):
+            grouped = pool.tile([P, N * PACK], BF16, name=name + "_grouped", align_bytes=64)
+            codes = pool.tile([P, N], U32, name=name + "_codes", align_bytes=64)
+            scales = pool.tile([P, N], U8, name=name + "_scales", align_bytes=64)
+            dealt = grouped[:].rearrange("p (t m j) -> p m j t", t=PACK, j=PACK)
+            for piece, (lo, mid, hi) in zip(raw, pieces):
+                columns = piece[:].rearrange("p j (m t) -> p m j t", t=PACK)
+                if lo < mid:
+                    round_on_scalar(dealt[:, lo:mid], columns[:, 0 : mid - lo], sign)
+                if mid < hi:
+                    round_on_vector(dealt[:, mid:hi], columns[:, mid - lo : hi - lo], sign)
+            for first in (0, HALF):
+                cols = slice(first, first + HALF)
+                nc.vector.quantize_mx(codes[:, cols].bitcast(FP8X4), scales[:, cols], grouped[:, first * PACK : (first + HALF) * PACK])
+            return codes, scales
+
+        def multiply(weight, t, name):
+            bank = psum.tile([P, S], F32, name="%s%d" % (name, t))
+            cols = slice(t * P, (t + 1) * P)
             nc.tensor.matmul_mx(
-                out,
-                lhsT=stationary[0].bitcast(FP8X4),
-                lhsT_scale=stationary[1],
-                rhs=moving[0].bitcast(FP8X4),
-                rhs_scale=moving[1],
+                bank[:],
+                lhsT=weight[0][:, cols].bitcast(FP8X4),
+                lhsT_scale=weight[1][:, cols],
+                rhs=x_code[:].bitcast(FP8X4),
+                rhs_scale=x_scale[:],
                 start=True,
                 stop=True,
             )
-
-        def by_features(weight, t, tag):
-            bank = psum.tile([P, S], F32, name="features_" + tag, tag=tag)
-            cols = slice(t * P, (t + 1) * P)
-            multiply(bank[:], (weight[0][:, cols], weight[1][:, cols]), (x_code[:], x_scale[:]))
             return bank
 
-        def by_tokens(weight, h, tag):
-            bank = psum.tile([P, 2, HALF], F32, name="tokens_" + tag, tag=tag)
-            for k in range(2):
-                tokens = slice(h * SPAN + k * P, h * SPAN + (k + 1) * P)
-                multiply(bank[:, k, :], (x_code[:, tokens], x_scale[:, tokens]), (weight[0][:, 0:HALF], weight[1][:, 0:HALF]))
-            return bank
+        w2_mx = prepare_weight("w2", w2_raw, W2_PIECES, 1.0)
+        gate_banks = [multiply(w2_mx, t, "gate") for t in range(PACK)]
+        w1_mx = prepare_weight("w1", w1_raw, W1_PIECES, -1.0)
+        layer_banks = [multiply(w1_mx, t, "layer") for t in range(PACK)]
 
-        def prepare_weight(name, raw, shares, firsts):
-            grouped, codes, scales = weight_tiles(name)
-            for piece, (lo, mid, hi) in zip(raw, shares):
-                deal(nc.scalar.copy, grouped, piece, lo, lo, mid)
-                if mid < hi:
-                    deal(nc.vector.tensor_copy, grouped, piece, lo, mid, hi)
-            for first in firsts:
-                quantise_columns(grouped, codes, scales, first, HALF)
-            return codes, scales
+        shut = pool.tile([P, PACK, S], F32, name="shut")
+        for t in range(PACK):
+            nc.scalar.activation(shut[:, t, :], gate_banks[t][:], ACT.Sigmoid, scale=-1.0)
 
-        w2_mx = prepare_weight("w2", w2_raw, W2_PIECES, (0, HALF))
-        gate_banks = [by_features(w2_mx, t, "bank%d" % t) for t in range(3)]
-        gate_turned_banks = [by_tokens(w2_mx, h, "bank%d" % (4 + h)) for h in range(2)]
-        gate_banks.append(by_features(w2_mx, 3, "bank3"))
-        w1_mx = prepare_weight("w1", w1_raw, W1_PIECES, (HALF, 0))
-        layer_banks = {2: by_features(w1_mx, 2, "bank6")}
-
-        gates = pool.tile([P, 2 * PACK, S], F32, name="gates", tag="w1_raw0")
-        shut = gates[:, 0:PACK, :]
-        gate_turned = gates[:, PACK : PACK + 2, :]
-        gate = {2: gates[:, PACK + 2, :], 3: gates[:, PACK + 3, :]}
-        shut_half = pool.tile([P, SPAN], F32, name="shut_half", tag="w1_raw1")
-
-        def close_gate(target, t, lo, hi):
-            nc.scalar.activation(target, gate_banks[t][:, lo:hi], ACT.Sigmoid, scale=-1.0)
-
-        def open_gate(target, bank):
-            nc.scalar.activation(target, bank, ACT.Sigmoid)
-
-        for t in (0, 1):
-            close_gate(shut[:, t, :], t, 0, S)
-        layer_turned_banks = [by_tokens(w1_mx, h, "bank%d" % h) for h in range(2)]
-        layer_banks[3] = by_features(w1_mx, 3, "bank7")
-        close_gate(shut_half[:], 2, 0, SPAN)
-        close_gate(shut[:, 2, SPAN:S], 2, SPAN, S)
-        open_gate(gate_turned[:, 0, :], gate_turned_banks[0][:].rearrange("p k c -> p (k c)"))
-        open_gate(gate[2], gate_banks[2][:])
-
+        picked = pool.tile([P, PACK, S], F32, name="picked")
         carried = pool.tile([P, PACK, S], F32, name="carried")
         result = pool.tile([P, PACK, S], F32, name="result")
         out_codes = pool.tile([P, S], U32, name="out_codes", align_bytes=64)
         out_scales = pool.tile([P, S], U8, name="out_scales", align_bytes=64)
         out_rows = out_0.rearrange("(p t) s -> p t s", t=PACK)
         out_words = out_1[0].rearrange("p s r -> p (s r)").bitcast(I32)
+        first, second = slice(0, SPAN), slice(SPAN, S)
 
-        def carry(t, closed, lo, hi):
-            picked = res_window[t][:].indirect(offsets[:, lo // 16 : hi // 16])
-            nc.vector.tensor_tensor(carried[:, t, lo:hi], picked, closed, ALU.mult)
+        def look_up(t, tokens):
+            return res_window[t][:].indirect(offsets[:, tokens.start // 16 : tokens.stop // 16])
 
-        def store(planes, lo, hi):
-            nc.sync.dma_start(out_rows[:, planes, lo:hi], result[:, planes, lo:hi])
+        def gate_layer(target, t, tokens):
+            nc.vector.scalar_tensor_tensor(target, shut[:, t, tokens], 1.0, layer_banks[t][:, tokens], ALU.subtract, ALU.mult)
+
+        def carry(engine, planes, tokens):
+            engine.tensor_tensor(carried[:, planes, tokens], picked[:, planes, tokens], shut[:, planes, tokens], ALU.mult)
+
+        def combine(planes, tokens, gated):
+            nc.vector.scalar_tensor_tensor(result[:, planes, tokens], gated, 0.0, carried[:, planes, tokens], ALU.max, ALU.add)
+
+        def store(planes, tokens):
+            nc.sync.dma_start(out_rows[:, planes, tokens], result[:, planes, tokens])
+
+        whole = slice(0, S)
+        for tokens in (first, second):
+            nc.vector.tensor_tensor(carried[:, 0, tokens], look_up(0, tokens), shut[:, 0, tokens], ALU.mult)
+        for tokens in (first, second):
+            gate_layer(shut[:, 0, tokens], 0, tokens)
+        for tokens in (first, second):
+            combine(0, tokens, shut[:, 0, tokens])
+        store(0, whole)
+
+        for t, tokens in ((1, whole), (2, whole), (3, first), (3, second)):
+            nc.scalar.activation(picked[:, t, tokens], look_up(t, tokens), ACT.Copy)
+
+        late = pool.tile([P, PACK - 1, S], F32, name="late", tag="res_window1")
+        carry(nc.gpsimd, 1, whole)
+        carry(nc.gpsimd, 2, first)
+        for t in range(1, PACK):
+            gate_layer(late[:, t - 1, :], t, whole)
+
+        carry(nc.vector, 3, first)
+        combine(slice(1, 3), first, late[:, 0:2, first])
+        combine(3, first, late[:, 2, first])
+        store(slice(1, 4), first)
+        carry(nc.vector, slice(2, 4), second)
+        combine(1, second, late[:, 0, second])
+        combine(slice(2, 4), second, late[:, 1:3, second])
+        store(slice(1, 4), second)
 
         grouped = [pool.tile([P, SPAN, PACK], BF16, name="out_grouped%d" % h, align_bytes=64) for h in range(2)]
 
@@ -169,65 +171,15 @@ def tile_picked_highway_relu_po_kernel(tc, x_words, x_scales, res, w1, w2, offs,
                 result[:, :, h * SPAN + lo : h * SPAN + hi].rearrange("p t (c i) -> p c t i", i=4),
             )
 
-        def quantise_out(h):
-            tokens = slice(h * SPAN, (h + 1) * SPAN)
+        def quantise_out(h, tokens):
             nc.vector.quantize_mx(out_codes[:, tokens].bitcast(FP8X4), out_scales[:, tokens], grouped[h][:].rearrange("p s t -> p (s t)"))
             nc.sync.dma_start(out_words[:, tokens], out_codes[:, tokens].bitcast(I32))
 
-        blocks = S // P
-        carried_turned = pool.tile([P, 2, blocks, P], F32, name="carried_turned")
-
-        def turn_carried(t, tag):
-            bank = psum.tile([P, blocks, P], F32, name="carried_bank%d" % t, tag=tag)
-            for k in range(blocks):
-                nc.tensor.transpose(bank[:, k, :], carried[:, t, k * P : (k + 1) * P], identity[:])
-            nc.scalar.copy(carried_turned[:, t], bank[:])
-
-        carry(0, shut[:, 0, :], 0, S)
-        turn_carried(0, "bank4")
-        open_gate(gate_turned[:, 1, :], gate_turned_banks[1][:].rearrange("p k c -> p (k c)"))
-        carry(1, shut[:, 1, :], 0, S)
-        turn_carried(1, "bank2")
-        open_gate(gate[3], gate_banks[3][:])
-        close_gate(shut[:, 3, :], 3, 0, S)
-        carry(2, shut_half[:], 0, SPAN)
-        carry(2, shut[:, 2, SPAN:S], SPAN, S)
-
-        products = pool.tile([P, PACK, S], F32, name="products", tag="w1_raw1")
-
-        def rectify(slot, bank, opened):
-            nc.vector.scalar_tensor_tensor(products[:, slot, :], bank, 0.0, opened, ALU.max, ALU.mult)
-
-        def add_turned(h, tag):
-            bank = psum.tile([P, 2, 2, P], F32, name="sum_bank%d" % h, tag=tag)
-            turned = products[:, h, :].rearrange("p (k t m) -> p k t m", k=2, t=2)
-            places = [(t, k) for t in range(2) for k in range(2)]
-            for i, (t, k) in enumerate(places):
-                nc.tensor.matmul(bank[:, t, k, :], carried_turned[:, t, 2 * h + k, :], identity[:], start=i == 0, stop=False, is_transpose=True)
-            for i, (t, k) in enumerate(places):
-                nc.tensor.matmul(bank[:, t, k, :], turned[:, k, t, :], identity[:], start=False, stop=i == len(places) - 1, is_transpose=True)
-            nc.scalar.copy(result[:, 0:2, h * SPAN : (h + 1) * SPAN], bank[:].rearrange("p t k c -> p t (k c)"))
-
-        rectify(2, layer_banks[2][:], gate[2])
-        nc.gpsimd.tensor_tensor(result[:, 2, :], products[:, 2, :], carried[:, 2, :], ALU.add)
-        store(2, 0, S)
-        for h in range(2):
-            rectify(h, layer_turned_banks[h][:].rearrange("p k c -> p (k c)"), gate_turned[:, h, :])
-        rectify(3, layer_banks[3][:], gate[3])
-        for h in range(2):
-            add_turned(h, "bank%d" % (5 - h))
-            store(slice(0, 2), h * SPAN, (h + 1) * SPAN)
-        for h in range(2):
-            carry(3, shut[:, 3, h * SPAN : (h + 1) * SPAN], h * SPAN, (h + 1) * SPAN)
-        for h in range(2):
-            tokens = slice(h * SPAN, (h + 1) * SPAN)
-            nc.vector.tensor_tensor(result[:, 3, tokens], products[:, 3, tokens], carried[:, 3, tokens], ALU.add)
-        store(3, 0, S)
-        interleave(nc.vector.tensor_copy, 0, 0, SPAN)
+        interleave(nc.scalar.copy, 0, 0, SPAN)
+        quantise_out(0, first)
         interleave(nc.scalar.copy, 1, 0, SCALAR_TOKENS)
         interleave(nc.vector.tensor_copy, 1, SCALAR_TOKENS, SPAN)
-        for h in range(2):
-            quantise_out(h)
+        quantise_out(1, second)
         for q in range(4):
             queue = nc.scalar if q % 2 else nc.sync
             queue.dma_start(out_2[0, 4 * q : 4 * q + 4, :].bitcast(I32), out_scales[32 * q : 32 * q + 4, :].bitcast(I32))

@@ -21,7 +21,8 @@ HALF = N // 2
 SPAN = S // 2
 W2_PIECES = ((0, 64, 64), (64, 90, 128))
 W1_PIECES = ((0, 0, 64), (64, 64, 96), (96, 96, 128))
-SCALAR_TOKENS = 96
+CHUNK_EDGES = (0, 160, 288, 384, 448, 512)
+FIRST_RUN = 384
 
 
 def tile_picked_highway_relu_po_kernel(tc, x_words, x_scales, res, w1, w2, offs, out_0, out_1, out_2):
@@ -119,7 +120,9 @@ def tile_picked_highway_relu_po_kernel(tc, x_words, x_scales, res, w1, w2, offs,
         out_scales = pool.tile([P, S], U8, name="out_scales", align_bytes=64)
         out_rows = out_0.rearrange("(p t) s -> p t s", t=PACK)
         out_words = out_1[0].rearrange("p s r -> p (s r)").bitcast(I32)
-        first, second = slice(0, SPAN), slice(SPAN, S)
+        first, second, whole = slice(0, SPAN), slice(SPAN, S), slice(0, S)
+        chunks = [slice(lo, hi) for lo, hi in zip(CHUNK_EDGES, CHUNK_EDGES[1:])]
+        runs = (slice(0, FIRST_RUN), slice(FIRST_RUN, S))
 
         def look_up(t, tokens):
             return res_window[t][:].indirect(offsets[:, tokens.start // 16 : tokens.stop // 16])
@@ -136,7 +139,6 @@ def tile_picked_highway_relu_po_kernel(tc, x_words, x_scales, res, w1, w2, offs,
         def store(planes, tokens):
             nc.sync.dma_start(out_rows[:, planes, tokens], result[:, planes, tokens])
 
-        whole = slice(0, S)
         for tokens in (first, second):
             nc.vector.tensor_tensor(carried[:, 0, tokens], look_up(0, tokens), shut[:, 0, tokens], ALU.mult)
         for tokens in (first, second):
@@ -145,41 +147,43 @@ def tile_picked_highway_relu_po_kernel(tc, x_words, x_scales, res, w1, w2, offs,
             combine(0, tokens, shut[:, 0, tokens])
         store(0, whole)
 
-        for t, tokens in ((1, whole), (2, whole), (3, first), (3, second)):
+        def pick(t, tokens):
             nc.scalar.activation(picked[:, t, tokens], look_up(t, tokens), ACT.Copy)
+
+        pick(1, whole)
+        pick(2, chunks[0])
+        pick(2, slice(chunks[0].stop, S))
+        for tokens in (chunks[0], chunks[1], slice(chunks[1].stop, S)):
+            pick(3, tokens)
 
         late = pool.tile([P, PACK - 1, S], F32, name="late", tag="res_window1")
         carry(nc.gpsimd, 1, whole)
-        carry(nc.gpsimd, 2, first)
+        carry(nc.gpsimd, 2, chunks[0])
         for t in range(1, PACK):
             gate_layer(late[:, t - 1, :], t, whole)
 
-        carry(nc.vector, 3, first)
-        combine(slice(1, 3), first, late[:, 0:2, first])
-        combine(3, first, late[:, 2, first])
-        store(slice(1, 4), first)
-        carry(nc.vector, slice(2, 4), second)
-        combine(1, second, late[:, 0, second])
-        combine(slice(2, 4), second, late[:, 1:3, second])
-        store(slice(1, 4), second)
+        grouped = [pool.tile([P, run.stop - run.start, PACK], BF16, name="out_grouped%d" % h, align_bytes=64) for h, run in enumerate(runs)]
 
-        grouped = [pool.tile([P, SPAN, PACK], BF16, name="out_grouped%d" % h, align_bytes=64) for h in range(2)]
-
-        def interleave(copy, h, lo, hi):
-            copy(
+        def finish(tokens):
+            combine(slice(1, PACK), tokens, late[:, :, tokens])
+            h = tokens.start // FIRST_RUN
+            lo, hi = tokens.start - runs[h].start, tokens.stop - runs[h].start
+            nc.scalar.copy(
                 grouped[h][:, lo:hi, :].rearrange("p (c i) t -> p c t i", i=4),
-                result[:, :, h * SPAN + lo : h * SPAN + hi].rearrange("p t (c i) -> p c t i", i=4),
+                result[:, :, tokens].rearrange("p t (c i) -> p c t i", i=4),
             )
+            if tokens.stop in (CHUNK_EDGES[2], S):
+                store(slice(1, PACK), slice(0, CHUNK_EDGES[2]) if tokens.stop < S else slice(CHUNK_EDGES[2], S))
 
-        def quantise_out(h, tokens):
-            nc.vector.quantize_mx(out_codes[:, tokens].bitcast(FP8X4), out_scales[:, tokens], grouped[h][:].rearrange("p s t -> p (s t)"))
-            nc.sync.dma_start(out_words[:, tokens], out_codes[:, tokens].bitcast(I32))
+        carry(nc.vector, 3, chunks[0])
+        for ahead, tokens in zip(chunks[1:], chunks):
+            carry(nc.vector, slice(2, PACK), ahead)
+            finish(tokens)
+        finish(chunks[-1])
 
-        interleave(nc.scalar.copy, 0, 0, SPAN)
-        quantise_out(0, first)
-        interleave(nc.scalar.copy, 1, 0, SCALAR_TOKENS)
-        interleave(nc.vector.tensor_copy, 1, SCALAR_TOKENS, SPAN)
-        quantise_out(1, second)
+        for h, run in enumerate(runs):
+            nc.vector.quantize_mx(out_codes[:, run].bitcast(FP8X4), out_scales[:, run], grouped[h][:].rearrange("p s t -> p (s t)"))
+            nc.sync.dma_start(out_words[:, run], out_codes[:, run].bitcast(I32))
         for q in range(4):
             queue = nc.scalar if q % 2 else nc.sync
             queue.dma_start(out_2[0, 4 * q : 4 * q + 4, :].bitcast(I32), out_scales[32 * q : 32 * q + 4, :].bitcast(I32))

@@ -56,9 +56,8 @@ def tile_picked_highway_relu_po_kernel(tc, x_words, x_scales, res, w1, w2, offs,
         word_window = pool.tile([P, T], U32, name="word_window")
         nc.sync.dma_start(word_window[:].bitcast(I32), x_words[0].rearrange("p c r -> p (c r)").bitcast(I32))
         nc.sync.dma_start(offsets[:], offs)
-        for q in range(4):
-            rows = x_scales[0, 4 * q : 4 * q + 4, :].bitcast(I32)
-            nc.sync.dma_start(scale_window[32 * q : 32 * q + 4, :].bitcast(I32), rows)
+        for r in range(4):
+            nc.sync.dma_start(scale_window[r:P:32, :].bitcast(I32), x_scales[0, r:16:4, :].bitcast(I32))
         w2_raw = load_weight(w2, "w2", W2_PIECES)
         w1_raw = load_weight(w1, "w1", W1_PIECES)
         res_window = [load_res(t) for t in range(PACK)]
@@ -184,6 +183,6 @@ def tile_picked_highway_relu_po_kernel(tc, x_words, x_scales, res, w1, w2, offs,
         for h, run in enumerate(runs):
             nc.vector.quantize_mx(out_codes[:, run].bitcast(FP8X4), out_scales[:, run], grouped[h][:].rearrange("p s t -> p (s t)"))
             nc.sync.dma_start(out_words[:, run], out_codes[:, run].bitcast(I32))
-        for q in range(4):
-            queue = nc.scalar if q % 2 else nc.sync
-            queue.dma_start(out_2[0, 4 * q : 4 * q + 4, :].bitcast(I32), out_scales[32 * q : 32 * q + 4, :].bitcast(I32))
+        for r in range(4):
+            queue = nc.scalar if r % 2 else nc.sync
+            queue.dma_start(out_2[0, r:16:4, :].bitcast(I32), out_scales[r:P:32, :].bitcast(I32))

from contextlib import ExitStack

import concourse.mybir as mybir

K, T, S, N = 512, 1024, 512, 512
FLOPS = 2 * 2 * K * N * S

F32 = mybir.dt.float32
BF16 = mybir.dt.bfloat16
I32 = mybir.dt.int32
U32 = mybir.dt.uint32
U16 = mybir.dt.uint16
U8 = mybir.dt.uint8
FP8X4 = mybir.dt.float8_e4m3fn_x4
ALU = mybir.AluOpType
ACT = mybir.ActivationFunctionType

P = 128
PACK = 4
HALF = N // 2
SPAN = S // 2
W2_PIECES = ((0, 64, 64), (64, 90, 128))
W1_PIECES = ((0, 0, 64), (64, 64, 96), (96, 96, 128))
CHUNK_EDGES = (0, 160, 288, 384, 448, 512)
FIRST_RUN = 384


def tile_picked_highway_relu_po_kernel(tc, x_words, x_scales, res, w1, w2, offs, out_0, out_1, out_2):
    nc = tc.nc
    with ExitStack() as ctx:
        pool = ctx.enter_context(tc.tile_pool(name="held", bufs=1))
        psum = ctx.enter_context(tc.psum_pool(name="psum", bufs=1))

        offsets = pool.tile([P, S // 16], U16, name="offsets")

        scale_window = pool.tile([P, T], U8, name="scale_window")
        nc.vector.memset(scale_window[:].bitcast(I32), 0)
        warm_in = pool.tile([P, 1], F32, name="warm_in")
        warm_out = pool.tile([P, 1], F32, name="warm_out")
        nc.vector.memset(warm_in[:], 0.0)
        nc.scalar.activation(warm_out[:], warm_in[:], ACT.Sigmoid)

        def load_weight(w, name, pieces):
            raws = []
            for h, (lo, mid, hi) in enumerate(pieces):
                raw = pool.tile([P, PACK, PACK * (hi - lo)], F32, name="%s_raw%d" % (name, h))
                nc.sync.dma_start(raw[:], w.rearrange("(p j) c -> p j c", j=PACK)[:, :, PACK * lo : PACK * hi])
                raws.append(raw)
            return raws

        def load_res(t):
            window = pool.tile([P, T], F32, name="res_window%d" % t, tag="res_window%d" % t)
            nc.sync.dma_start(window[:], res.rearrange("(p t) c -> p t c", t=PACK)[:, t, :])
            return window

        word_window = pool.tile([P, T], U32, name="word_window")
        nc.sync.dma_start(word_window[:].bitcast(I32), x_words[0].rearrange("p c r -> p (c r)").bitcast(I32))
        nc.sync.dma_start(offsets[:], offs)
        for r in range(4):
            nc.sync.dma_start(scale_window[r:P:32, :].bitcast(I32), x_scales[0, r:16:4, :].bitcast(I32))
        w2_raw = load_weight(w2, "w2", W2_PIECES)
        w1_raw = load_weight(w1, "w1", W1_PIECES)
        res_window = [load_res(t) for t in range(PACK)]

        x_code = pool.tile([P, S], U32, name="x_code", align_bytes=64)
        nc.vector.tensor_copy(x_code[:], word_window[:].indirect(offsets[:]))
        x_scale = pool.tile([P, S], U8, name="x_scale", align_bytes=64)
        nc.vector.tensor_copy(x_scale[:], scale_window[:].indirect(offsets[:]))

        def round_on_scalar(target, source, sign):
            nc.scalar.activation(target, source, ACT.Copy, scale=sign)

        def round_on_vector(target, source, sign):
            nc.vector.tensor_scalar(target, source, sign, None, ALU.mult)

        def prepare_weight(name, raw, pieces, sign):
            grouped = pool.tile([P, N * PACK], BF16, name=name + "_grouped", align_bytes=64)
            codes = pool.tile([P, N], U32, name=name + "_codes", align_bytes=64)
            scales = pool.tile([P, N], U8, name=name + "_scales", align_bytes=64)
            dealt = grouped[:].rearrange("p (t m j) -> p m j t", t=PACK, j=PACK)
            for piece, (lo, mid, hi) in zip(raw, pieces):
                columns = piece[:].rearrange("p j (m t) -> p m j t", t=PACK)
                if lo < mid:
                    round_on_scalar(dealt[:, lo:mid], columns[:, 0 : mid - lo], sign)
                if mid < hi:
                    round_on_vector(dealt[:, mid:hi], columns[:, mid - lo : hi - lo], sign)
            for first in (0, HALF):
                cols = slice(first, first + HALF)
                nc.vector.quantize_mx(codes[:, cols].bitcast(FP8X4), scales[:, cols], grouped[:, first * PACK : (first + HALF) * PACK])
            return codes, scales

        def multiply(weight, t, name):
            bank = psum.tile([P, S], F32, name="%s%d" % (name, t))
            cols = slice(t * P, (t + 1) * P)
            nc.tensor.matmul_mx(
                bank[:],
                lhsT=weight[0][:, cols].bitcast(FP8X4),
                lhsT_scale=weight[1][:, cols],
                rhs=x_code[:].bitcast(FP8X4),
                rhs_scale=x_scale[:],
                start=True,
                stop=True,
            )
            return bank

        w2_mx = prepare_weight("w2", w2_raw, W2_PIECES, 1.0)
        gate_banks = [multiply(w2_mx, t, "gate") for t in range(PACK)]
        w1_mx = prepare_weight("w1", w1_raw, W1_PIECES, -1.0)
        layer_banks = [multiply(w1_mx, t, "layer") for t in range(PACK)]

        shut = pool.tile([P, PACK, S], F32, name="shut")
        for t in range(PACK):
            nc.scalar.activation(shut[:, t, :], gate_banks[t][:], ACT.Sigmoid, scale=-1.0)

        picked = pool.tile([P, PACK, S], F32, name="picked")
        carried = pool.tile([P, PACK, S], F32, name="carried")
        result = pool.tile([P, PACK, S], F32, name="result")
        out_codes = pool.tile([P, S], U32, name="out_codes", align_bytes=64)
        out_scales = pool.tile([P, S], U8, name="out_scales", align_bytes=64)
        out_rows = out_0.rearrange("(p t) s -> p t s", t=PACK)
        out_words = out_1[0].rearrange("p s r -> p (s r)").bitcast(I32)
        first, second, whole = slice(0, SPAN), slice(SPAN, S), slice(0, S)
        chunks = [slice(lo, hi) for lo, hi in zip(CHUNK_EDGES, CHUNK_EDGES[1:])]
        runs = (slice(0, FIRST_RUN), slice(FIRST_RUN, S))

        def look_up(t, tokens):
            return res_window[t][:].indirect(offsets[:, tokens.start // 16 : tokens.stop // 16])

        def gate_layer(target, t, tokens):
            nc.vector.scalar_tensor_tensor(target, shut[:, t, tokens], 1.0, layer_banks[t][:, tokens], ALU.subtract, ALU.mult)

        def carry(engine, planes, tokens):
            engine.tensor_tensor(carried[:, planes, tokens], picked[:, planes, tokens], shut[:, planes, tokens], ALU.mult)

        def combine(planes, tokens, gated):
            nc.vector.scalar_tensor_tensor(result[:, planes, tokens], gated, 0.0, carried[:, planes, tokens], ALU.max, ALU.add)

        def store(planes, tokens):
            nc.sync.dma_start(out_rows[:, planes, tokens], result[:, planes, tokens])

        for tokens in (first, second):
            nc.vector.tensor_tensor(carried[:, 0, tokens], look_up(0, tokens), shut[:, 0, tokens], ALU.mult)
        for tokens in (first, second):
            gate_layer(shut[:, 0, tokens], 0, tokens)
        for tokens in (first, second):
            combine(0, tokens, shut[:, 0, tokens])
        store(0, whole)

        def pick(t, tokens):
            nc.scalar.activation(picked[:, t, tokens], look_up(t, tokens), ACT.Copy)

        pick(1, whole)
        pick(2, chunks[0])
        pick(2, slice(chunks[0].stop, S))
        for tokens in (chunks[0], chunks[1], slice(chunks[1].stop, S)):
            pick(3, tokens)

        late = pool.tile([P, PACK - 1, S], F32, name="late", tag="res_window1")
        carry(nc.gpsimd, 1, whole)
        carry(nc.gpsimd, 2, chunks[0])
        for t in range(1, PACK):
            gate_layer(late[:, t - 1, :], t, whole)

        grouped = [pool.tile([P, run.stop - run.start, PACK], BF16, name="out_grouped%d" % h, align_bytes=64) for h, run in enumerate(runs)]

        def finish(tokens):
            combine(slice(1, PACK), tokens, late[:, :, tokens])
            h = tokens.start // FIRST_RUN
            lo, hi = tokens.start - runs[h].start, tokens.stop - runs[h].start
            nc.scalar.copy(
                grouped[h][:, lo:hi, :].rearrange("p (c i) t -> p c t i", i=4),
                result[:, :, tokens].rearrange("p t (c i) -> p c t i", i=4),
            )
            if tokens.stop in (CHUNK_EDGES[2], S):
                store(slice(1, PACK), slice(0, CHUNK_EDGES[2]) if tokens.stop < S else slice(CHUNK_EDGES[2], S))

        carry(nc.vector, 3, chunks[0])
        for ahead, tokens in zip(chunks[1:], chunks):
            carry(nc.vector, slice(2, PACK), ahead)
            finish(tokens)
        finish(chunks[-1])

        for h, run in enumerate(runs):
            nc.vector.quantize_mx(out_codes[:, run].bitcast(FP8X4), out_scales[:, run], grouped[h][:].rearrange("p s t -> p (s t)"))
            nc.sync.dma_start(out_words[:, run], out_codes[:, run].bitcast(I32))
        for r in range(4):
            queue = nc.scalar if r % 2 else nc.sync
            queue.dma_start(out_2[0, r:16:4, :].bitcast(I32), out_scales[r:P:32, :].bitcast(I32))
